import numpy as np
import ml_dtypes


def mxq(x, axis, fmt="e4m3"):
    dtype, down = {"e4m3": (ml_dtypes.float8_e4m3fn, 7), "e5m2": (ml_dtypes.float8_e5m2, 14)}[fmt]
    v = np.moveaxis(np.asarray(x, np.float32).astype(ml_dtypes.bfloat16).astype(np.float64), axis, -1)
    blocks = v.reshape(v.shape[:-1] + (-1, 32))
    amax = np.abs(blocks).max(-1, keepdims=True)
    byte = np.maximum(np.where(amax > 0, np.frexp(amax)[1] - 1 + 127, 0) - down, 1)
    scale = np.exp2(byte - 127.0)
    codes = (blocks / scale).astype(np.float32).astype(dtype).astype(np.float64)
    return np.moveaxis((codes * scale).reshape(v.shape), -1, axis)


WIDE = False


def mx_kscale(k):
    if not WIDE:
        return np.ones(k)
    levels = np.array([10, -10, 5, -5, 0])
    if k % 512:
        return np.exp2(np.random.permutation(np.resize(levels, k // 32))).repeat(32)
    a = np.empty((k // 512, 16))
    for p in range(k // 512):
        a[p, :8] = np.random.permutation(np.resize(levels, 8))
        for g in range(8):
            far = levels[np.abs(levels - a[p, g]) >= 10]
            a[p, g + 8] = far[np.random.randint(len(far))]
    return np.exp2(a.ravel()).repeat(32)


def f64(x):
    return np.asarray(x).astype(np.float64)


def striped(idx):
    return np.tile(np.asarray(idx).reshape(-1, 16).T, (8, 1)).astype(np.uint16)


def unstriped(offs):
    return offs[:16].T.reshape(-1).astype(np.int64)


E2M1 = np.array([0.0, 0.5, 1.0, 1.5, 2.0, 3.0, 4.0, 6.0, -0.0, -0.5, -1.0, -1.5, -2.0, -3.0, -4.0, -6.0])


def pack_weight(w, fmt):
    k, n = w.shape
    w = f64(np.asarray(w, np.float32).astype(ml_dtypes.bfloat16)).reshape(k // 32, 32, n)
    amax = np.abs(w).max(1)
    if fmt == "e4m3":
        byte = np.frexp(amax)[1] - 1 + 127 - 7
    else:
        mant, ex = np.frexp(amax / 6.0)
        byte = np.where(mant > 0.5, ex, ex - 1) + 127
    byte = np.clip(np.where(amax > 0, byte, 1), 1, 254)
    scaled = (w * np.exp2(127.0 - byte)[:, None, :]).reshape(k, n).astype(np.float32)
    by_word = np.ascontiguousarray(scaled.reshape(k // 512, 128, 4, n).transpose(0, 1, 3, 2))
    if fmt == "e4m3":
        words = by_word.astype(ml_dtypes.float8_e4m3fn).view(np.uint8)
    else:
        c = by_word.astype(ml_dtypes.float4_e2m1fn).view(np.uint8) & 0xF
        words = (c[..., 0::2] | (c[..., 1::2] << 4)).reshape(k // 512, 128, 2 * n)
    return np.ascontiguousarray(words), np.ascontiguousarray(byte.astype(np.uint8).reshape(k // 512, 16, n))


def unpack_weight(words, scales, fmt):
    g, _, n = scales.shape
    words = np.ascontiguousarray(words).reshape(g, 128, n, -1)
    if fmt == "e4m3":
        vals = words.view(ml_dtypes.float8_e4m3fn).astype(np.float64)
    else:
        nib = np.empty((g, 128, n, 4), np.uint8)
        nib[..., 0::2] = words & 0xF
        nib[..., 1::2] = words >> 4
        vals = E2M1[nib]
    vals = vals * np.repeat(np.exp2(scales.astype(np.float64) - 127.0), 8, axis=1)[..., None]
    return vals.transpose(0, 1, 3, 2).reshape(g * 512, n)


def sigmoid(v):
    return 1.0 / (1.0 + np.exp(-v))


def bf(x):
    return np.asarray(x, np.float32).astype(ml_dtypes.bfloat16)


def planes(Y):
    r, m = Y.shape
    b = f64(bf(Y)).reshape(r // 32, 32, m)
    amax = np.abs(b).max(1)
    byte = np.clip(np.where(amax > 0, np.frexp(amax)[1] - 1 + 127 - 7, 1), 1, 254)
    codes = (b * np.exp2(127.0 - byte)[:, None, :]).reshape(r, m).astype(np.float32).astype(ml_dtypes.float8_e4m3fn).view(np.uint8)
    words = codes.reshape(r // 512, 128, 4, m).transpose(0, 1, 3, 2)
    return np.ascontiguousarray(words), np.ascontiguousarray(byte.astype(np.uint8).reshape(r // 512, 16, m))


B, N, T, D, NQ = 1, 512, 2048, 1024, 512
DV = 512


def sgn(shape):
    return np.random.uniform(0.5, 2.0, shape) * np.where(np.random.standard_normal(shape) < 0, -1.0, 1.0)


def setup_inputs():
    n = np.random.standard_normal
    idx = np.random.permutation(T)[:B * N]
    s = mx_kscale(D)[:, None]
    u = mx_kscale(N)
    ut = np.ones(T)
    ut[idx] = u
    kp = pack_weight(n((D, T)) / s, "e2m1")
    return {
        "qT": (n((B, D, NQ)) * s * (1.00 / np.sqrt(D))).astype(np.float32),
        "k_words": np.ascontiguousarray(kp[0].reshape(1, 2, 128, T, 2).transpose(0, 2, 3, 1, 4)).reshape(1, 128, T, 4),
        "k_scales": kp[1],
        "vT": (n((DV, T)) / ut).astype(np.float32),
        "th": (n((B, 1, NQ)) + 1).astype(np.float32),
        "og": (n((B, DV, NQ))).astype(np.float32),
        "us": (sgn((B, N, 1)) * u[:, None]).astype(np.float32),
        "offs": striped(idx),
    }


def reference(qT, k_words, k_scales, vT, th, og, us, offs):
    idx = unstriped(offs)
    pick = lambda x, which: x[:, which].reshape(x.shape[0], B, -1).transpose(1, 0, 2)
    k = unpack_weight(k_words.reshape(1, 128, T, 2, 2).transpose(0, 3, 1, 2, 4).reshape(2, 128, 2 * T), k_scales, "e2m1")
    kg = pick(k, idx)
    qq = mxq(f64(qT), 1, "e4m3")
    a = kg.transpose(0, 2, 1) @ qq
    y = sigmoid(a - f64(th)) * f64(us)
    wq = mxq(y, 1, "e4m3")
    o = mxq(pick(f64(vT), idx).transpose(0, 2, 1), 1, "e4m3").transpose(0, 2, 1) @ wq
    r_ = o * sigmoid(f64(og))
    Y = r_[0]
    words, scales = planes(Y)
    return Y, words, scales

@@ -1,0 +1,246 @@
+from contextlib import ExitStack
+
+import concourse.mybir as mybir
+from concourse.masks import make_identity
+
+F32 = mybir.dt.float32
+BF16 = mybir.dt.bfloat16
+I32 = mybir.dt.int32
+U32 = mybir.dt.uint32
+U16 = mybir.dt.uint16
+U8 = mybir.dt.uint8
+FP8X4 = mybir.dt.float8_e4m3fn_x4
+FP4X4 = mybir.dt.float4_e2m1fn_x4
+MULT = mybir.AluOpType.mult
+SIGMOID = mybir.ActivationFunctionType.Sigmoid
+
+P = 128
+PACK = 4
+D, T, N, NQ, DV = 1024, 2048, 512, 512, 512
+PASSES = D // (P * PACK)
+HALF = NQ // 2
+
+FLOPS = 2 * N * NQ * (D + DV)
+
+
+def interleave(copy, dst, src):
+    copy(dst.rearrange("p (c i) t -> p c t i", i=4), src.rearrange("p t (c i) -> p c t i", i=4))
+
+
+def quantize(nc, codes, scales, grouped):
+    nc.vector.quantize_mx(out=codes.bitcast(FP8X4), scales=scales, in_=grouped.rearrange("p c t -> p (c t)"))
+
+
+def tile_attend_plo_siggate_topk_kernel(tc, qT, k_words, k_scales, vT, th, og, us, offs, out_0, out_1, out_2):
+    nc = tc.nc
+    with ExitStack() as ctx:
+        sb = ctx.enter_context(tc.tile_pool(name="sb", bufs=1))
+        ps = ctx.enter_context(tc.psum_pool(name="ps", bufs=1))
+
+        def tile(name, shape, dtype, tag=None):
+            return sb.tile(shape, dtype, name=name, tag=tag or name, align_bytes=64)
+
+        offsets = tile("offsets", [P, N // 16], U16)
+        ks_pool = tile("ks_pool", [P, T], U8)
+        ks = [tile("ks%d" % g, [P, N], U8) for g in range(PASSES)]
+        th_rows = tile("th_rows", [P, P], F32)
+        ident = tile("ident", [P, P], F32)
+        nc.vector.memset(ks_pool[32:64, :].bitcast(I32), 0)
+        nc.vector.memset(ks_pool[64:128, :].bitcast(I32), 0)
+        for g in range(PASSES):
+            nc.vector.memset(ks[g][:].bitcast(I32), 0)
+        nc.gpsimd.memset(th_rows[:], 0.0)
+        make_identity(nc, ident[:])
+
+        q_raw = [tile("q_raw%d" % g, [P, PACK, NQ], F32) for g in range(PASSES)]
+        kw_pool = tile("kw_pool", [P, T], I32)
+        us_sb = tile("us_sb", [P, PACK], F32)
+        v_pool = [tile("v_pool%d" % t, [P, T], F32) for t in range(PACK)]
+        og_sb = [tile("og_sb%d" % t, [P, NQ], F32) for t in range(PACK)]
+
+        q_rows = qT[0].rearrange("(g p t) q -> g p t q", p=P, t=PACK)
+        nc.sync.dma_start(offsets[:], offs)
+        nc.sync.dma_start(ks_pool[0:32, :].bitcast(I32), k_scales.rearrange("o f t -> (o f) t").bitcast(I32))
+        nc.sync.dma_start(kw_pool[:], k_words[0].rearrange("p t b -> p (t b)").bitcast(I32))
+        for g in range(PASSES):
+            nc.sync.dma_start(q_raw[g][:], q_rows[g])
+        nc.scalar.dma_start(us_sb[:], us[0].rearrange("(p r) one -> p (r one)", r=PACK))
+        nc.scalar.dma_start(th_rows[0:4, :], th[0, 0].rearrange("(j p) -> j p", p=P))
+        v_rows = vT.rearrange("(p t) n -> t p n", t=PACK)
+        og_rows = og[0].rearrange("(p t) q -> t p q", t=PACK)
+        for t in range(PACK):
+            nc.sync.dma_start(v_pool[t][:], v_rows[t])
+        for t in range(PACK):
+            nc.sync.dma_start(og_sb[t][:], og_rows[t])
+
+        th_ps = ps.tile([P, P], F32, name="th_ps", tag="vt", bufs=2)
+        nc.tensor.transpose(th_ps[:], th_rows[:], ident[:])
+        neg_th = tile("neg_th", [P, NQ // P], F32)
+        nc.vector.tensor_scalar(neg_th[:], th_ps[:, 0 : NQ // P], -1.0, None, MULT)
+
+        ks_picked = tile("ks_picked", [P, N], U8)
+        nc.vector.tensor_copy(ks_picked[:], ks_pool[:].indirect(offsets[:]))
+        for g in range(PASSES):
+            for quad in range(4):
+                row = 16 * g + 4 * quad
+                nc.scalar.dma_start(
+                    ks[g][32 * quad : 32 * quad + 4, :].bitcast(I32), ks_picked[row : row + 4, :].bitcast(I32)
+                )
+        kw = tile("kw", [P, N], U32)
+        nc.vector.tensor_copy(kw[:], kw_pool[:].bitcast(U32).indirect(offsets[:]))
+        k_codes = [tile("k_codes%d" % g, [P, 2 * N], U8) for g in range(PASSES)]
+        for g in range(PASSES):
+            nc.vector.tensor_copy(k_codes[g][:].bitcast(U16), kw[:].bitcast(U16)[:, g : 2 * N : 2])
+
+        q_codes = [[tile("q_codes%d%d" % (g, h), [P, HALF], U32) for h in range(2)] for g in range(PASSES)]
+        q_scales = [[tile("q_scales%d%d" % (g, h), [P, HALF], U8) for h in range(2)] for g in range(PASSES)]
+        for g in range(PASSES):
+            q_grp = [tile("q_grp%d%d" % (g, h), [P, HALF, PACK], BF16) for h in range(2)]
+            for h, copy in enumerate((nc.vector.tensor_copy, nc.scalar.copy)):
+                interleave(copy, q_grp[h][:], q_raw[g][:, :, h * HALF : (h + 1) * HALF])
+            for h in range(2):
+                quantize(nc, q_codes[g][h][:], q_scales[g][h][:], q_grp[h][:])
+
+        score = [ps.tile([P, N], F32, name="score%d" % j, tag="acc%d" % j) for j in range(4)]
+        for g in range(PASSES):
+            for j in range(4):
+                h, c = divmod(j, 2)
+                nc.tensor.matmul_mx(
+                    score[j][:],
+                    lhsT=q_codes[g][h][:, c * P : (c + 1) * P].bitcast(FP8X4),
+                    lhsT_scale=q_scales[g][h][:, c * P : (c + 1) * P],
+                    rhs=k_codes[g][:].bitcast(FP4X4),
+                    rhs_scale=ks[g][:],
+                    start=(g == 0),
+                    stop=(g == PASSES - 1),
+                )
+
+        v_codes = {}
+        v_grp = {}
+        v_turned = {}
+        v_scales = [tile("v_scales%d" % t, [P, P], U8) for t in range(PACK)]
+
+        def v_tile(t):
+            picked = tile("v_picked%d" % t, [P, N], BF16)
+            nc.vector.tensor_copy(picked[:], v_pool[t][:].indirect(offsets[:]))
+            words = picked[:].bitcast(F32)
+            turned = ps.tile([P, 2, P], F32, name="v_turned%d" % t, tag="vt", bufs=2)
+            for u in range(2):
+                nc.tensor.transpose(turned[:, u, :], words[:, u : 2 * P : 2], ident[:])
+            v_turned[t] = turned
+
+        def v_copy(t, tag=None):
+            turned = v_turned[t]
+            grouped = tile("v_grp%d" % t, [P, P, PACK], BF16, tag=tag)
+            nc.scalar.copy(
+                grouped[:].rearrange("p c t -> p (c t)").bitcast(F32).rearrange("p (c u) -> p c u", u=2),
+                turned[:].rearrange("p u c -> p c u"),
+            )
+            v_grp[t] = grouped
+
+        def v_quant(t):
+            v_codes[t] = tile("v_codes%d" % t, [P, P], U32, tag=("v_picked1", "v_pool2", "v_pool3", None)[t])
+            quantize(nc, v_codes[t][:], v_scales[t][:], v_grp[t][:])
+
+        y_grp = {}
+        y_codes = tile("y_codes", [P, NQ], U32)
+        y_scales = tile("y_scales", [P, NQ], U8)
+
+        def y_block(j):
+            h, c = divmod(j, 2)
+            if c == 0:
+                y_grp[h] = tile("y_grp%d" % h, [P, HALF, PACK], BF16, tag="v_pool%d" % h)
+            sig = tile("sig%d" % j, [P, PACK, P], F32)
+            nc.scalar.activation(
+                sig[:], score[j][:].rearrange("p (s r) -> p r s", r=PACK), SIGMOID, bias=neg_th[:, j : j + 1]
+            )
+            turned = ps.tile([P, PACK, P], F32, name="y_turned%d" % j, tag="yt", bufs=2)
+            for r in range(PACK):
+                nc.tensor.transpose(turned[:, r, :], sig[:, r, :], ident[:])
+            nc.vector.tensor_tensor(
+                y_grp[h][:, c * P : (c + 1) * P, :],
+                turned[:].rearrange("p r q -> p q r"),
+                us_sb[:].unsqueeze(1).broadcast_to([P, P, PACK]),
+                MULT,
+            )
+
+        def y_quant(h):
+            cols = slice(h * HALF, (h + 1) * HALF)
+            quantize(nc, y_codes[:, cols], y_scales[:, cols], y_grp[h][:])
+
+        gates = {}
+
+        def gate_tile(t):
+            gates[t] = tile("gate%d" % t, [P, NQ], F32)
+            nc.scalar.activation(gates[t][:], og_sb[t][:], SIGMOID)
+
+        v_tile(0)
+        y_block(0)
+        y_block(1)
+        v_copy(0)
+        v_tile(1)
+        y_block(2)
+        y_quant(0)
+        y_block(3)
+        v_copy(1)
+        v_quant(0)
+        y_quant(1)
+        v_tile(2)
+        v_copy(2)
+        v_quant(1)
+        v_tile(3)
+        v_quant(2)
+        gate_tile(0)
+        gate_tile(1)
+        v_copy(3, tag="og_sb1")
+        v_quant(3)
+        gate_tile(2)
+        gate_tile(3)
+
+        def product(acc, t, cols):
+            nc.tensor.matmul_mx(
+                acc,
+                lhsT=v_codes[t][:].bitcast(FP8X4),
+                lhsT_scale=v_scales[t][:],
+                rhs=y_codes[:, cols].bitcast(FP8X4),
+                rhs_scale=y_scales[:, cols],
+                start=True,
+                stop=True,
+            )
+
+        res = [tile("res%d" % h, [P, PACK, HALF], F32) for h in range(2)]
+        out_rows = out_0.rearrange("(p t) q -> p t q", t=PACK)
+        halves = [slice(h * HALF, (h + 1) * HALF) for h in range(2)]
+        for t in range(PACK):
+            gate = gates[t]
+            if t < PACK - 1:
+                acc = ps.tile([P, NQ], F32, name="o%d" % t, tag="acc%d" % t)
+                product(acc[:], t, slice(0, NQ))
+                sums = [acc[:, cols] for cols in halves]
+            else:
+                first = ps.tile([P, HALF], F32, name="o_first", tag="acc%d" % t)
+                second = ps.tile([P, HALF], F32, name="o_second", tag="yt", bufs=2)
+                sums = [first[:], second[:]]
+                for h in range(2):
+                    product(sums[h], t, halves[h])
+            for h in range(2):
+                nc.vector.tensor_tensor(res[h][:, t, :], sums[h], gate[:, halves[h]], MULT)
+            if t % 2 == 1:
+                for h in range(2):
+                    nc.sync.dma_start(out_rows[:, t - 1 : t + 1, halves[h]], res[h][:, t - 1 : t + 1, :])
+
+        o_scales = tile("o_scales", [P, NQ], U8)
+        words_out = out_1[0].rearrange("p q b -> p (q b)").bitcast(I32)
+        o_grp = [tile("o_grp%d" % h, [P, HALF, PACK], BF16) for h in range(2)]
+        interleave(nc.scalar.copy, o_grp[0][:], res[0][:])
+        interleave(nc.vector.tensor_copy, o_grp[1][:], res[1][:])
+        for h in (1, 0):
+            o_codes = tile("o_codes%d" % h, [P, HALF], U32)
+            quantize(nc, o_codes[:], o_scales[:, halves[h]], o_grp[h][:])
+            nc.sync.dma_start(words_out[:, halves[h]], o_codes[:].bitcast(I32))
+        for quad in range(4):
+            queue = nc.scalar if quad % 2 == 0 else nc.sync
+            queue.dma_start(
+                out_2[0, 4 * quad : 4 * quad + 4, :].bitcast(I32),
+                o_scales[32 * quad : 32 * quad + 4, :].bitcast(I32),
+            )

@@ -12,6 +12,7 @@ U8 = mybir.dt.uint8
 FP8X4 = mybir.dt.float8_e4m3fn_x4
 FP4X4 = mybir.dt.float4_e2m1fn_x4
 MULT = mybir.AluOpType.mult
+COPY = mybir.ActivationFunctionType.Copy
 SIGMOID = mybir.ActivationFunctionType.Sigmoid
 
 P = 128
@@ -19,6 +20,8 @@ PACK = 4
 D, T, N, NQ, DV = 1024, 2048, 512, 512, 512
 PASSES = D // (P * PACK)
 HALF = NQ // 2
+
+HEAD = 64
 
 FLOPS = 2 * N * NQ * (D + DV)
 
@@ -56,22 +59,21 @@ def tile_attend_plo_siggate_topk_kernel(tc, qT, k_words, k_scales, vT, th, og, u
         kw_pool = tile("kw_pool", [P, T], I32)
         us_sb = tile("us_sb", [P, PACK], F32)
         v_pool = [tile("v_pool%d" % t, [P, T], F32) for t in range(PACK)]
-        og_sb = [tile("og_sb%d" % t, [P, NQ], F32) for t in range(PACK)]
+        og_head = tile("og_head", [P, HEAD], F32)
+        og_first = [HEAD, 0, 0, 0]
+        og_sb = [tile("og_sb%d" % t, [P, NQ - og_first[t]], F32) for t in range(PACK)]
+        gates = [tile("gate%d" % t, [P, NQ], F32) for t in range(PACK)]
 
         q_rows = qT[0].rearrange("(g p t) q -> g p t q", p=P, t=PACK)
         nc.sync.dma_start(offsets[:], offs)
         nc.sync.dma_start(ks_pool[0:32, :].bitcast(I32), k_scales.rearrange("o f t -> (o f) t").bitcast(I32))
         nc.sync.dma_start(kw_pool[:], k_words[0].rearrange("p t b -> p (t b)").bitcast(I32))
-        for g in range(PASSES):
-            nc.sync.dma_start(q_raw[g][:], q_rows[g])
         nc.scalar.dma_start(us_sb[:], us[0].rearrange("(p r) one -> p (r one)", r=PACK))
         nc.scalar.dma_start(th_rows[0:4, :], th[0, 0].rearrange("(j p) -> j p", p=P))
         v_rows = vT.rearrange("(p t) n -> t p n", t=PACK)
         og_rows = og[0].rearrange("(p t) q -> t p q", t=PACK)
-        for t in range(PACK):
-            nc.sync.dma_start(v_pool[t][:], v_rows[t])
-        for t in range(PACK):
-            nc.sync.dma_start(og_sb[t][:], og_rows[t])
+        nc.scalar.dma_start(og_head[:], og_rows[0][:, 0:HEAD])
+        nc.scalar.activation(gates[0][:, 0:HEAD], og_head[:], SIGMOID)
 
         th_ps = ps.tile([P, P], F32, name="th_ps", tag="vt", bufs=2)
         nc.tensor.transpose(th_ps[:], th_rows[:], ident[:])
@@ -81,11 +83,16 @@ def tile_attend_plo_siggate_topk_kernel(tc, qT, k_words, k_scales, vT, th, og, u
         ks_picked = tile("ks_picked", [P, N], U8)
         nc.vector.tensor_copy(ks_picked[:], ks_pool[:].indirect(offsets[:]))
         for g in range(PASSES):
+            nc.sync.dma_start(q_raw[g][:], q_rows[g])
             for quad in range(4):
                 row = 16 * g + 4 * quad
-                nc.scalar.dma_start(
+                nc.sync.dma_start(
                     ks[g][32 * quad : 32 * quad + 4, :].bitcast(I32), ks_picked[row : row + 4, :].bitcast(I32)
                 )
+        for t in range(PACK):
+            nc.sync.dma_start(v_pool[t][:], v_rows[t])
+        for t in range(PACK):
+            nc.sync.dma_start(og_sb[t][:], og_rows[t][:, og_first[t] : NQ])
         kw = tile("kw", [P, N], U32)
         nc.vector.tensor_copy(kw[:], kw_pool[:].bitcast(U32).indirect(offsets[:]))
         k_codes = [tile("k_codes%d" % g, [P, 2 * N], U8) for g in range(PASSES)]
@@ -115,41 +122,46 @@ def tile_attend_plo_siggate_topk_kernel(tc, qT, k_words, k_scales, vT, th, og, u
                     stop=(g == PASSES - 1),
                 )
 
-        v_codes = {}
-        v_grp = {}
         v_turned = {}
-        v_scales = [tile("v_scales%d" % t, [P, P], U8) for t in range(PACK)]
+        v_codes = {}
+        v_scales = {}
 
-        def v_tile(t):
+        def v_turn(t, picked):
+            words = picked[:].bitcast(F32)
+            v_turned[t] = ps.tile([P, 2, P], F32, name="v_turned%d" % t, tag="vt", bufs=2)
+            for u in range(2):
+                nc.tensor.transpose(v_turned[t][:, u, :], words[:, u : 2 * P : 2], ident[:])
+
+        def v_pick(t):
             picked = tile("v_picked%d" % t, [P, N], BF16)
             nc.vector.tensor_copy(picked[:], v_pool[t][:].indirect(offsets[:]))
-            words = picked[:].bitcast(F32)
-            turned = ps.tile([P, 2, P], F32, name="v_turned%d" % t, tag="vt", bufs=2)
-            for u in range(2):
-                nc.tensor.transpose(turned[:, u, :], words[:, u : 2 * P : 2], ident[:])
-            v_turned[t] = turned
+            v_turn(t, picked)
 
-        def v_copy(t, tag=None):
-            turned = v_turned[t]
-            grouped = tile("v_grp%d" % t, [P, P, PACK], BF16, tag=tag)
-            nc.scalar.copy(
-                grouped[:].rearrange("p c t -> p (c t)").bitcast(F32).rearrange("p (c u) -> p c u", u=2),
-                turned[:].rearrange("p u c -> p c u"),
+        def v_pick_on_scalar(t):
+            rounded = tile("v_rounded%d" % t, [P, T], BF16)
+            nc.scalar.activation(rounded[:], v_pool[t][:], COPY)
+            picked = tile("v_picked%d" % t, [P, N], BF16)
+            nc.scalar.activation(picked[:], rounded[:].indirect(offsets[:]), COPY)
+            v_turn(t, picked)
+
+        def v_copy(t, grouped, copy=nc.scalar.copy):
+            copy(
+                grouped.rearrange("p c t -> p (c t)").bitcast(F32).rearrange("p (c u) -> p c u", u=2),
+                v_turned[t][:].rearrange("p u c -> p c u"),
             )
-            v_grp[t] = grouped
 
-        def v_quant(t):
-            v_codes[t] = tile("v_codes%d" % t, [P, P], U32, tag=("v_picked1", "v_pool2", "v_pool3", None)[t])
-            quantize(nc, v_codes[t][:], v_scales[t][:], v_grp[t][:])
+        def v_quant(first, grouped, count, tag=None):
+            codes = tile("v_codes%d" % first, [P, count * P], U32, tag=tag)
+            scales = tile("v_scales%d" % first, [P, count * P], U8)
+            quantize(nc, codes[:], scales[:], grouped[:])
+            for i in range(count):
+                v_codes[first + i] = codes[:, i * P : (i + 1) * P]
+                v_scales[first + i] = scales[:, i * P : (i + 1) * P]
 
-        y_grp = {}
         y_codes = tile("y_codes", [P, NQ], U32)
         y_scales = tile("y_scales", [P, NQ], U8)
 
         def y_block(j):
-            h, c = divmod(j, 2)
-            if c == 0:
-                y_grp[h] = tile("y_grp%d" % h, [P, HALF, PACK], BF16, tag="v_pool%d" % h)
             sig = tile("sig%d" % j, [P, PACK, P], F32)
             nc.scalar.activation(
                 sig[:], score[j][:].rearrange("p (s r) -> p r s", r=PACK), SIGMOID, bias=neg_th[:, j : j + 1]
@@ -158,57 +170,51 @@ def tile_attend_plo_siggate_topk_kernel(tc, qT, k_words, k_scales, vT, th, og, u
             for r in range(PACK):
                 nc.tensor.transpose(turned[:, r, :], sig[:, r, :], ident[:])
             nc.vector.tensor_tensor(
-                y_grp[h][:, c * P : (c + 1) * P, :],
+                y_grp[:, j * P : (j + 1) * P, :],
                 turned[:].rearrange("p r q -> p q r"),
                 us_sb[:].unsqueeze(1).broadcast_to([P, P, PACK]),
                 MULT,
             )
 
-        def y_quant(h):
-            cols = slice(h * HALF, (h + 1) * HALF)
-            quantize(nc, y_codes[:, cols], y_scales[:, cols], y_grp[h][:])
-
-        gates = {}
-
         def gate_tile(t):
-            gates[t] = tile("gate%d" % t, [P, NQ], F32)
-            nc.scalar.activation(gates[t][:], og_sb[t][:], SIGMOID)
+            nc.scalar.activation(gates[t][:, og_first[t] : NQ], og_sb[t][:], SIGMOID)
 
-        v_tile(0)
-        y_block(0)
-        y_block(1)
-        v_copy(0)
-        v_tile(1)
-        y_block(2)
-        y_quant(0)
-        y_block(3)
-        v_copy(1)
-        v_quant(0)
-        y_quant(1)
-        v_tile(2)
-        v_copy(2)
-        v_quant(1)
-        v_tile(3)
-        v_quant(2)
+        v_pick(0)
+        y_grp = tile("y_grp", [P, NQ, PACK], BF16, tag="v_pool0")
+        for j in range(4):
+            y_block(j)
+        quantize(nc, y_codes[:], y_scales[:], y_grp[:])
+        v_grp0 = tile("v_grp0", [P, P, PACK], BF16)
+        v_copy(0, v_grp0[:])
+        v_quant(0, v_grp0, 1)
+        v_pick_on_scalar(1)
+        v_pick(2)
+        v_grp12 = tile("v_grp12", [P, 2 * P, PACK], BF16)
+        v_copy(1, v_grp12[:, 0:P, :])
+        v_copy(2, v_grp12[:, P : 2 * P, :], nc.vector.tensor_copy)
+        v_pick(3)
+        v_quant(1, v_grp12, 2, tag="v_pool3")
         gate_tile(0)
         gate_tile(1)
-        v_copy(3, tag="og_sb1")
-        v_quant(3)
+        v_grp3 = tile("v_grp3", [P, P, PACK], BF16, tag="og_sb1")
+        v_copy(3, v_grp3[:])
+        v_quant(3, v_grp3, 1)
         gate_tile(2)
         gate_tile(3)
 
         def product(acc, t, cols):
             nc.tensor.matmul_mx(
                 acc,
-                lhsT=v_codes[t][:].bitcast(FP8X4),
-                lhsT_scale=v_scales[t][:],
+                lhsT=v_codes[t].bitcast(FP8X4),
+                lhsT_scale=v_scales[t],
                 rhs=y_codes[:, cols].bitcast(FP8X4),
                 rhs_scale=y_scales[:, cols],
                 start=True,
                 stop=True,
             )
 
-        res = [tile("res%d" % h, [P, PACK, HALF], F32) for h in range(2)]
+        res_all = tile("res_all", [P, 2, PACK, HALF], F32)
+        res = [res_all[:, h] for h in range(2)]
         out_rows = out_0.rearrange("(p t) q -> p t q", t=PACK)
         halves = [slice(h * HALF, (h + 1) * HALF) for h in range(2)]
         for t in range(PACK):
@@ -216,15 +222,20 @@ def tile_attend_plo_siggate_topk_kernel(tc, qT, k_words, k_scales, vT, th, og, u
             if t < PACK - 1:
                 acc = ps.tile([P, NQ], F32, name="o%d" % t, tag="acc%d" % t)
                 product(acc[:], t, slice(0, NQ))
-                sums = [acc[:, cols] for cols in halves]
+                nc.vector.tensor_tensor(
+                    res_all[:, :, t, :],
+                    acc[:].rearrange("p (h c) -> p h c", h=2),
+                    gate[:].rearrange("p (h c) -> p h c", h=2),
+                    MULT,
+                )
             else:
                 first = ps.tile([P, HALF], F32, name="o_first", tag="acc%d" % t)
                 second = ps.tile([P, HALF], F32, name="o_second", tag="yt", bufs=2)
                 sums = [first[:], second[:]]
                 for h in range(2):
                     product(sums[h], t, halves[h])
-            for h in range(2):
-                nc.vector.tensor_tensor(res[h][:, t, :], sums[h], gate[:, halves[h]], MULT)
+                for h in range(2):
+                    nc.vector.tensor_tensor(res[h][:, t, :], sums[h], gate[:, halves[h]], MULT)
             if t % 2 == 1:
                 for h in range(2):
                     nc.sync.dma_start(out_rows[:, t - 1 : t + 1, halves[h]], res[h][:, t - 1 : t + 1, :])
@@ -232,8 +243,8 @@ def tile_attend_plo_siggate_topk_kernel(tc, qT, k_words, k_scales, vT, th, og, u
         o_scales = tile("o_scales", [P, NQ], U8)
         words_out = out_1[0].rearrange("p q b -> p (q b)").bitcast(I32)
         o_grp = [tile("o_grp%d" % h, [P, HALF, PACK], BF16) for h in range(2)]
-        interleave(nc.scalar.copy, o_grp[0][:], res[0][:])
-        interleave(nc.vector.tensor_copy, o_grp[1][:], res[1][:])
+        interleave(nc.scalar.copy, o_grp[0][:], res[0])
+        interleave(nc.vector.tensor_copy, o_grp[1][:], res[1])
         for h in (1, 0):
             o_codes = tile("o_codes%d" % h, [P, HALF], U32)
             quantize(nc, o_codes[:], o_scales[:, halves[h]], o_grp[h][:])

@@ -144,8 +144,8 @@ def tile_attend_plo_siggate_topk_kernel(tc, qT, k_words, k_scales, vT, th, og, u
             nc.scalar.activation(picked[:], rounded[:].indirect(offsets[:]), COPY)
             v_turn(t, picked)
 
-        def v_copy(t, grouped, copy=nc.scalar.copy):
-            copy(
+        def v_copy(t, grouped):
+            nc.scalar.copy(
                 grouped.rearrange("p c t -> p (c t)").bitcast(F32).rearrange("p (c u) -> p c u", u=2),
                 v_turned[t][:].rearrange("p u c -> p c u"),
             )
@@ -191,14 +191,14 @@ def tile_attend_plo_siggate_topk_kernel(tc, qT, k_words, k_scales, vT, th, og, u
         v_pick(2)
         v_grp12 = tile("v_grp12", [P, 2 * P, PACK], BF16)
         v_copy(1, v_grp12[:, 0:P, :])
-        v_copy(2, v_grp12[:, P : 2 * P, :], nc.vector.tensor_copy)
+        v_copy(2, v_grp12[:, P : 2 * P, :])
         v_pick(3)
         v_quant(1, v_grp12, 2, tag="v_pool3")
         gate_tile(0)
-        gate_tile(1)
-        v_grp3 = tile("v_grp3", [P, P, PACK], BF16, tag="og_sb1")
+        v_grp3 = tile("v_grp3", [P, P, PACK], BF16, tag="og_sb0")
         v_copy(3, v_grp3[:])
         v_quant(3, v_grp3, 1)
+        gate_tile(1)
         gate_tile(2)
         gate_tile(3)
 

@@ -22,6 +22,7 @@ PASSES = D // (P * PACK)
 HALF = NQ // 2
 
 HEAD = 64
+SCALAR_COLS = 192
 
 FLOPS = 2 * N * NQ * (D + DV)
 
@@ -126,23 +127,26 @@ def tile_attend_plo_siggate_topk_kernel(tc, qT, k_words, k_scales, vT, th, og, u
         v_codes = {}
         v_scales = {}
 
-        def v_turn(t, picked):
-            words = picked[:].bitcast(F32)
+        def v_turn(t, word_sets):
             v_turned[t] = ps.tile([P, 2, P], F32, name="v_turned%d" % t, tag="vt", bufs=2)
             for u in range(2):
-                nc.tensor.transpose(v_turned[t][:, u, :], words[:, u : 2 * P : 2], ident[:])
+                nc.tensor.transpose(v_turned[t][:, u, :], word_sets[u], ident[:])
 
         def v_pick(t):
             picked = tile("v_picked%d" % t, [P, N], BF16)
             nc.vector.tensor_copy(picked[:], v_pool[t][:].indirect(offsets[:]))
-            v_turn(t, picked)
+            words = picked[:].bitcast(F32)
+            v_turn(t, [words[:, u : 2 * P : 2] for u in range(2)])
 
         def v_pick_on_scalar(t):
             rounded = tile("v_rounded%d" % t, [P, T], BF16)
             nc.scalar.activation(rounded[:], v_pool[t][:], COPY)
             picked = tile("v_picked%d" % t, [P, N], BF16)
-            nc.scalar.activation(picked[:], rounded[:].indirect(offsets[:]), COPY)
-            v_turn(t, picked)
+            nc.scalar.activation(
+                picked[:].rearrange("p (u s e) -> p s u e", u=2, e=2), rounded[:].indirect(offsets[:]), COPY
+            )
+            words = picked[:].bitcast(F32)
+            v_turn(t, [words[:, u * P : (u + 1) * P] for u in range(2)])
 
         def v_copy(t, grouped):
             nc.scalar.copy(
@@ -243,9 +247,10 @@ def tile_attend_plo_siggate_topk_kernel(tc, qT, k_words, k_scales, vT, th, og, u
         o_scales = tile("o_scales", [P, NQ], U8)
         words_out = out_1[0].rearrange("p q b -> p (q b)").bitcast(I32)
         o_grp = [tile("o_grp%d" % h, [P, HALF, PACK], BF16) for h in range(2)]
-        interleave(nc.scalar.copy, o_grp[0][:], res[0])
+        interleave(nc.scalar.copy, o_grp[0][:, 0:SCALAR_COLS, :], res[0][:, :, 0:SCALAR_COLS])
+        interleave(nc.vector.tensor_copy, o_grp[0][:, SCALAR_COLS:HALF, :], res[0][:, :, SCALAR_COLS:HALF])
         interleave(nc.vector.tensor_copy, o_grp[1][:], res[1])
-        for h in (1, 0):
+        for h in range(2):
             o_codes = tile("o_codes%d" % h, [P, HALF], U32)
             quantize(nc, o_codes[:], o_scales[:, halves[h]], o_grp[h][:])
             nc.sync.dma_start(words_out[:, halves[h]], o_codes[:].bitcast(I32))

@@ -183,14 +183,39 @@ def tile_attend_plo_siggate_topk_kernel(tc, qT, k_words, k_scales, vT, th, og, u
         def gate_tile(t):
             nc.scalar.activation(gates[t][:, og_first[t] : NQ], og_sb[t][:], SIGMOID)
 
+        def product(acc, t, cols):
+            nc.tensor.matmul_mx(
+                acc,
+                lhsT=v_codes[t].bitcast(FP8X4),
+                lhsT_scale=v_scales[t],
+                rhs=y_codes[:, cols].bitcast(FP8X4),
+                rhs_scale=y_scales[:, cols],
+                start=True,
+                stop=True,
+            )
+
         v_pick(0)
         y_grp = tile("y_grp", [P, NQ, PACK], BF16, tag="v_pool0")
         for j in range(4):
             y_block(j)
+        warm = ps.tile([P, N], F32, name="warm", tag="yt", bufs=2)
+        for g in range(PASSES):
+            nc.tensor.matmul_mx(
+                warm[:],
+                lhsT=q_codes[g][0][:, 0:P].bitcast(FP8X4),
+                lhsT_scale=q_scales[g][0][:, 0:P],
+                rhs=k_codes[g][:].bitcast(FP4X4),
+                rhs_scale=ks[g][:],
+                start=(g == 0),
+                stop=(g == PASSES - 1),
+            )
         quantize(nc, y_codes[:], y_scales[:], y_grp[:])
+        accs = [ps.tile([P, NQ], F32, name="o%d" % t, tag="acc%d" % t) for t in range(PACK - 1)]
         v_grp0 = tile("v_grp0", [P, P, PACK], BF16)
         v_copy(0, v_grp0[:])
         v_quant(0, v_grp0, 1)
+        product(accs[0][:], 0, slice(0, NQ))
+        product(accs[1][:], 0, slice(0, NQ))
         v_pick_on_scalar(1)
         v_pick(2)
         v_grp12 = tile("v_grp12", [P, 2 * P, PACK], BF16)
@@ -206,17 +231,6 @@ def tile_attend_plo_siggate_topk_kernel(tc, qT, k_words, k_scales, vT, th, og, u
         gate_tile(2)
         gate_tile(3)
 
-        def product(acc, t, cols):
-            nc.tensor.matmul_mx(
-                acc,
-                lhsT=v_codes[t].bitcast(FP8X4),
-                lhsT_scale=v_scales[t],
-                rhs=y_codes[:, cols].bitcast(FP8X4),
-                rhs_scale=y_scales[:, cols],
-                start=True,
-                stop=True,
-            )
-
         res_all = tile("res_all", [P, 2, PACK, HALF], F32)
         res = [res_all[:, h] for h in range(2)]
         out_rows = out_0.rearrange("(p t) q -> p t q", t=PACK)
@@ -224,8 +238,9 @@ def tile_attend_plo_siggate_topk_kernel(tc, qT, k_words, k_scales, vT, th, og, u
         for t in range(PACK):
             gate = gates[t]
             if t < PACK - 1:
-                acc = ps.tile([P, NQ], F32, name="o%d" % t, tag="acc%d" % t)
-                product(acc[:], t, slice(0, NQ))
+                acc = accs[t]
+                if t > 0:
+                    product(acc[:], t, slice(0, NQ))
                 nc.vector.tensor_tensor(
                     res_all[:, :, t, :],
                     acc[:].rearrange("p (h c) -> p h c", h=2),

@@ -62,7 +62,13 @@ def tile_attend_plo_siggate_topk_kernel(tc, qT, k_words, k_scales, vT, th, og, u
         v_pool = [tile("v_pool%d" % t, [P, T], F32) for t in range(PACK)]
         og_head = tile("og_head", [P, HEAD], F32)
         og_first = [HEAD, 0, 0, 0]
-        og_sb = [tile("og_sb%d" % t, [P, NQ - og_first[t]], F32) for t in range(PACK)]
+        og_pair = [tile("og_pair0", [P, 2 * NQ - HEAD], F32), tile("og_pair1", [P, 2 * NQ], F32)]
+        og_sb = [
+            og_pair[0][:, 0 : NQ - HEAD],
+            og_pair[0][:, NQ - HEAD : 2 * NQ - HEAD],
+            og_pair[1][:, 0:NQ],
+            og_pair[1][:, NQ : 2 * NQ],
+        ]
         gates = [tile("gate%d" % t, [P, NQ], F32) for t in range(PACK)]
 
         q_rows = qT[0].rearrange("(g p t) q -> g p t q", p=P, t=PACK)
@@ -92,8 +98,9 @@ def tile_attend_plo_siggate_topk_kernel(tc, qT, k_words, k_scales, vT, th, og, u
                 )
         for t in range(PACK):
             nc.sync.dma_start(v_pool[t][:], v_rows[t])
-        for t in range(PACK):
-            nc.sync.dma_start(og_sb[t][:], og_rows[t][:, og_first[t] : NQ])
+        og_flat = og[0].rearrange("(p t) q -> p (t q)", t=PACK)
+        nc.sync.dma_start(og_pair[0][:], og_flat[:, HEAD : 2 * NQ])
+        nc.sync.dma_start(og_pair[1][:], og_flat[:, 2 * NQ : 4 * NQ])
         kw = tile("kw", [P, N], U32)
         nc.vector.tensor_copy(kw[:], kw_pool[:].bitcast(U32).indirect(offsets[:]))
         k_codes = [tile("k_codes%d" % g, [P, 2 * N], U8) for g in range(PASSES)]
@@ -181,7 +188,7 @@ def tile_attend_plo_siggate_topk_kernel(tc, qT, k_words, k_scales, vT, th, og, u
             )
 
         def gate_tile(t):
-            nc.scalar.activation(gates[t][:, og_first[t] : NQ], og_sb[t][:], SIGMOID)
+            nc.scalar.activation(gates[t][:, og_first[t] : NQ], og_sb[t], SIGMOID)
 
         def product(acc, t, cols):
             nc.tensor.matmul_mx(
@@ -224,29 +231,23 @@ def tile_attend_plo_siggate_topk_kernel(tc, qT, k_words, k_scales, vT, th, og, u
         v_pick(3)
         v_quant(1, v_grp12, 2, tag="v_pool3")
         gate_tile(0)
-        v_grp3 = tile("v_grp3", [P, P, PACK], BF16, tag="og_sb0")
+        v_grp3 = tile("v_grp3", [P, P, PACK], BF16, tag="og_pair0")
         v_copy(3, v_grp3[:])
         v_quant(3, v_grp3, 1)
         gate_tile(1)
         gate_tile(2)
         gate_tile(3)
 
-        res_all = tile("res_all", [P, 2, PACK, HALF], F32)
-        res = [res_all[:, h] for h in range(2)]
-        out_rows = out_0.rearrange("(p t) q -> p t q", t=PACK)
         halves = [slice(h * HALF, (h + 1) * HALF) for h in range(2)]
+        res = tile("res", [P, PACK, NQ], F32)
+        out_rows = out_0.rearrange("(p t) q -> p t q", t=PACK)
         for t in range(PACK):
             gate = gates[t]
             if t < PACK - 1:
                 acc = accs[t]
                 if t > 0:
                     product(acc[:], t, slice(0, NQ))
-                nc.vector.tensor_tensor(
-                    res_all[:, :, t, :],
-                    acc[:].rearrange("p (h c) -> p h c", h=2),
-                    gate[:].rearrange("p (h c) -> p h c", h=2),
-                    MULT,
-                )
+                nc.vector.tensor_tensor(res[:, t, :], acc[:], gate[:], MULT)
             else:
                 first = ps.tile([P, HALF], F32, name="o_first", tag="acc%d" % t)
                 second = ps.tile([P, HALF], F32, name="o_second", tag="yt", bufs=2)
@@ -254,17 +255,15 @@ def tile_attend_plo_siggate_topk_kernel(tc, qT, k_words, k_scales, vT, th, og, u
                 for h in range(2):
                     product(sums[h], t, halves[h])
                 for h in range(2):
-                    nc.vector.tensor_tensor(res[h][:, t, :], sums[h], gate[:, halves[h]], MULT)
-            if t % 2 == 1:
-                for h in range(2):
-                    nc.sync.dma_start(out_rows[:, t - 1 : t + 1, halves[h]], res[h][:, t - 1 : t + 1, :])
+                    nc.vector.tensor_tensor(res[:, t, halves[h]], sums[h], gate[:, halves[h]], MULT)
+            nc.sync.dma_start(out_rows[:, t, :], res[:, t, :])
 
         o_scales = tile("o_scales", [P, NQ], U8)
         words_out = out_1[0].rearrange("p q b -> p (q b)").bitcast(I32)
         o_grp = [tile("o_grp%d" % h, [P, HALF, PACK], BF16) for h in range(2)]
-        interleave(nc.scalar.copy, o_grp[0][:, 0:SCALAR_COLS, :], res[0][:, :, 0:SCALAR_COLS])
-        interleave(nc.vector.tensor_copy, o_grp[0][:, SCALAR_COLS:HALF, :], res[0][:, :, SCALAR_COLS:HALF])
-        interleave(nc.vector.tensor_copy, o_grp[1][:], res[1])
+        interleave(nc.scalar.copy, o_grp[0][:, 0:SCALAR_COLS, :], res[:, :, 0:SCALAR_COLS])
+        interleave(nc.vector.tensor_copy, o_grp[0][:, SCALAR_COLS:HALF, :], res[:, :, SCALAR_COLS:HALF])
+        interleave(nc.vector.tensor_copy, o_grp[1][:], res[:, :, halves[1]])
         for h in range(2):
             o_codes = tile("o_codes%d" % h, [P, HALF], U32)
             quantize(nc, o_codes[:], o_scales[:, halves[h]], o_grp[h][:])

@@ -21,7 +21,6 @@ D, T, N, NQ, DV = 1024, 2048, 512, 512, 512
 PASSES = D // (P * PACK)
 HALF = NQ // 2
 
-HEAD = 64
 SCALAR_COLS = 192
 
 FLOPS = 2 * N * NQ * (D + DV)
@@ -53,39 +52,38 @@ def tile_attend_plo_siggate_topk_kernel(tc, qT, k_words, k_scales, vT, th, og, u
         nc.vector.memset(ks_pool[64:128, :].bitcast(I32), 0)
         for g in range(PASSES):
             nc.vector.memset(ks[g][:].bitcast(I32), 0)
+        us_rows = tile("us_rows", [P, N], F32)
         nc.gpsimd.memset(th_rows[:], 0.0)
+        nc.gpsimd.memset(us_rows[:], 0.0)
         make_identity(nc, ident[:])
 
         q_raw = [tile("q_raw%d" % g, [P, PACK, NQ], F32) for g in range(PASSES)]
         kw_pool = tile("kw_pool", [P, T], I32)
         us_sb = tile("us_sb", [P, PACK], F32)
         v_pool = [tile("v_pool%d" % t, [P, T], F32) for t in range(PACK)]
-        og_head = tile("og_head", [P, HEAD], F32)
-        og_first = [HEAD, 0, 0, 0]
-        og_pair = [tile("og_pair0", [P, 2 * NQ - HEAD], F32), tile("og_pair1", [P, 2 * NQ], F32)]
-        og_sb = [
-            og_pair[0][:, 0 : NQ - HEAD],
-            og_pair[0][:, NQ - HEAD : 2 * NQ - HEAD],
-            og_pair[1][:, 0:NQ],
-            og_pair[1][:, NQ : 2 * NQ],
-        ]
+        og_tiles = [tile("og0", [P, 1, NQ], F32), tile("og1", [P, 1, NQ], F32), tile("og23", [P, 2, NQ], F32)]
+        og_sb = [og_tiles[0][:, 0, :], og_tiles[1][:, 0, :], og_tiles[2][:, 0, :], og_tiles[2][:, 1, :]]
         gates = [tile("gate%d" % t, [P, NQ], F32) for t in range(PACK)]
 
         q_rows = qT[0].rearrange("(g p t) q -> g p t q", p=P, t=PACK)
         nc.sync.dma_start(offsets[:], offs)
         nc.sync.dma_start(ks_pool[0:32, :].bitcast(I32), k_scales.rearrange("o f t -> (o f) t").bitcast(I32))
         nc.sync.dma_start(kw_pool[:], k_words[0].rearrange("p t b -> p (t b)").bitcast(I32))
-        nc.scalar.dma_start(us_sb[:], us[0].rearrange("(p r) one -> p (r one)", r=PACK))
         nc.scalar.dma_start(th_rows[0:4, :], th[0, 0].rearrange("(j p) -> j p", p=P))
+        nc.scalar.dma_start(us_rows[0:1, :], us[0].rearrange("n one -> one n"))
         v_rows = vT.rearrange("(p t) n -> t p n", t=PACK)
-        og_rows = og[0].rearrange("(p t) q -> t p q", t=PACK)
-        nc.scalar.dma_start(og_head[:], og_rows[0][:, 0:HEAD])
-        nc.scalar.activation(gates[0][:, 0:HEAD], og_head[:], SIGMOID)
+        table_warm = tile("table_warm", [P, 1], F32)
+        nc.scalar.activation(table_warm[64:128, :], th_rows[64:128, 0:1], SIGMOID)
 
         th_ps = ps.tile([P, P], F32, name="th_ps", tag="vt", bufs=2)
         nc.tensor.transpose(th_ps[:], th_rows[:], ident[:])
         neg_th = tile("neg_th", [P, NQ // P], F32)
-        nc.vector.tensor_scalar(neg_th[:], th_ps[:, 0 : NQ // P], -1.0, None, MULT)
+        nc.scalar.activation(neg_th[:], th_ps[:, 0 : NQ // P], COPY, scale=-1.0)
+
+        us_ps = ps.tile([P, PACK, P], F32, name="us_ps", tag="vt", bufs=2)
+        for r in range(PACK):
+            nc.tensor.transpose(us_ps[:, r, :], us_rows[:, r:N:PACK], ident[:])
+        nc.scalar.copy(us_sb[:], us_ps[:, :, 0])
 
         ks_picked = tile("ks_picked", [P, N], U8)
         nc.vector.tensor_copy(ks_picked[:], ks_pool[:].indirect(offsets[:]))
@@ -98,9 +96,9 @@ def tile_attend_plo_siggate_topk_kernel(tc, qT, k_words, k_scales, vT, th, og, u
                 )
         for t in range(PACK):
             nc.sync.dma_start(v_pool[t][:], v_rows[t])
-        og_flat = og[0].rearrange("(p t) q -> p (t q)", t=PACK)
-        nc.sync.dma_start(og_pair[0][:], og_flat[:, HEAD : 2 * NQ])
-        nc.sync.dma_start(og_pair[1][:], og_flat[:, 2 * NQ : 4 * NQ])
+        og_rows = og[0].rearrange("(p t) q -> p t q", t=PACK)
+        for og_tile, rows in zip(og_tiles, (slice(0, 1), slice(1, 2), slice(2, 4))):
+            nc.sync.dma_start(og_tile[:], og_rows[:, rows, :])
         kw = tile("kw", [P, N], U32)
         nc.vector.tensor_copy(kw[:], kw_pool[:].bitcast(U32).indirect(offsets[:]))
         k_codes = [tile("k_codes%d" % g, [P, 2 * N], U8) for g in range(PASSES)]
@@ -188,7 +186,7 @@ def tile_attend_plo_siggate_topk_kernel(tc, qT, k_words, k_scales, vT, th, og, u
             )
 
         def gate_tile(t):
-            nc.scalar.activation(gates[t][:, og_first[t] : NQ], og_sb[t], SIGMOID)
+            nc.scalar.activation(gates[t][:], og_sb[t], SIGMOID)
 
         def product(acc, t, cols):
             nc.tensor.matmul_mx(
@@ -231,7 +229,7 @@ def tile_attend_plo_siggate_topk_kernel(tc, qT, k_words, k_scales, vT, th, og, u
         v_pick(3)
         v_quant(1, v_grp12, 2, tag="v_pool3")
         gate_tile(0)
-        v_grp3 = tile("v_grp3", [P, P, PACK], BF16, tag="og_pair0")
+        v_grp3 = tile("v_grp3", [P, P, PACK], BF16, tag="og0")
         v_copy(3, v_grp3[:])
         v_quant(3, v_grp3, 1)
         gate_tile(1)

@@ -128,6 +128,7 @@ def tile_attend_plo_siggate_topk_kernel(tc, qT, k_words, k_scales, vT, th, og, u
                     stop=(g == PASSES - 1),
                 )
 
+        halves = [slice(h * HALF, (h + 1) * HALF) for h in range(2)]
         v_turned = {}
         v_codes = {}
         v_scales = {}
@@ -201,8 +202,10 @@ def tile_attend_plo_siggate_topk_kernel(tc, qT, k_words, k_scales, vT, th, og, u
 
         v_pick(0)
         y_grp = tile("y_grp", [P, NQ, PACK], BF16, tag="v_pool0")
-        for j in range(4):
-            y_block(j)
+        for h in range(2):
+            y_block(2 * h)
+            y_block(2 * h + 1)
+            quantize(nc, y_codes[:, halves[h]], y_scales[:, halves[h]], y_grp[:, halves[h], :])
         warm = ps.tile([P, N], F32, name="warm", tag="yt", bufs=2)
         for g in range(PASSES):
             nc.tensor.matmul_mx(
@@ -214,7 +217,6 @@ def tile_attend_plo_siggate_topk_kernel(tc, qT, k_words, k_scales, vT, th, og, u
                 start=(g == 0),
                 stop=(g == PASSES - 1),
             )
-        quantize(nc, y_codes[:], y_scales[:], y_grp[:])
         accs = [ps.tile([P, NQ], F32, name="o%d" % t, tag="acc%d" % t) for t in range(PACK - 1)]
         v_grp0 = tile("v_grp0", [P, P, PACK], BF16)
         v_copy(0, v_grp0[:])
@@ -236,7 +238,6 @@ def tile_attend_plo_siggate_topk_kernel(tc, qT, k_words, k_scales, vT, th, og, u
         gate_tile(2)
         gate_tile(3)
 
-        halves = [slice(h * HALF, (h + 1) * HALF) for h in range(2)]
         res = tile("res", [P, PACK, NQ], F32)
         out_rows = out_0.rearrange("(p t) q -> p t q", t=PACK)
         for t in range(PACK):

@@ -206,23 +206,11 @@ def tile_attend_plo_siggate_topk_kernel(tc, qT, k_words, k_scales, vT, th, og, u
             y_block(2 * h)
             y_block(2 * h + 1)
             quantize(nc, y_codes[:, halves[h]], y_scales[:, halves[h]], y_grp[:, halves[h], :])
-        warm = ps.tile([P, N], F32, name="warm", tag="yt", bufs=2)
-        for g in range(PASSES):
-            nc.tensor.matmul_mx(
-                warm[:],
-                lhsT=q_codes[g][0][:, 0:P].bitcast(FP8X4),
-                lhsT_scale=q_scales[g][0][:, 0:P],
-                rhs=k_codes[g][:].bitcast(FP4X4),
-                rhs_scale=ks[g][:],
-                start=(g == 0),
-                stop=(g == PASSES - 1),
-            )
         accs = [ps.tile([P, NQ], F32, name="o%d" % t, tag="acc%d" % t) for t in range(PACK - 1)]
         v_grp0 = tile("v_grp0", [P, P, PACK], BF16)
         v_copy(0, v_grp0[:])
         v_quant(0, v_grp0, 1)
         product(accs[0][:], 0, slice(0, NQ))
-        product(accs[1][:], 0, slice(0, NQ))
         v_pick_on_scalar(1)
         v_pick(2)
         v_grp12 = tile("v_grp12", [P, 2 * P, PACK], BF16)

@@ -40,8 +40,13 @@ def tile_attend_plo_siggate_topk_kernel(tc, qT, k_words, k_scales, vT, th, og, u
         sb = ctx.enter_context(tc.tile_pool(name="sb", bufs=1))
         ps = ctx.enter_context(tc.psum_pool(name="ps", bufs=1))
 
+        shared = ctx.enter_context(tc.tile_pool(name="shared", bufs=1))
+
         def tile(name, shape, dtype, tag=None):
             return sb.tile(shape, dtype, name=name, tag=tag or name, align_bytes=64)
+
+        def placed(name, shape, dtype, offset):
+            return shared.tile(shape, dtype, name=name, tag=name, align_bytes=64, offset=offset)
 
         offsets = tile("offsets", [P, N // 16], U16)
         ks_pool = tile("ks_pool", [P, T], U8)
@@ -50,8 +55,9 @@ def tile_attend_plo_siggate_topk_kernel(tc, qT, k_words, k_scales, vT, th, og, u
         ident = tile("ident", [P, P], F32)
         nc.vector.memset(ks_pool[32:64, :].bitcast(I32), 0)
         nc.vector.memset(ks_pool[64:128, :].bitcast(I32), 0)
-        for g in range(PASSES):
-            nc.vector.memset(ks[g][:].bitcast(I32), 0)
+        nc.vector.memset(ks[0][32:64, :].bitcast(I32), 0)
+        nc.vector.memset(ks[0][64:128, :].bitcast(I32), 0)
+        nc.vector.memset(ks[1][:].bitcast(I32), 0)
         us_rows = tile("us_rows", [P, N], F32)
         nc.gpsimd.memset(th_rows[:], 0.0)
         nc.gpsimd.memset(us_rows[:], 0.0)
@@ -60,9 +66,10 @@ def tile_attend_plo_siggate_topk_kernel(tc, qT, k_words, k_scales, vT, th, og, u
         q_raw = [tile("q_raw%d" % g, [P, PACK, NQ], F32) for g in range(PASSES)]
         kw_pool = tile("kw_pool", [P, T], I32)
         us_sb = tile("us_sb", [P, PACK], F32)
-        v_pool = [tile("v_pool%d" % t, [P, T], F32) for t in range(PACK)]
-        og_tiles = [tile("og0", [P, 1, NQ], F32), tile("og1", [P, 1, NQ], F32), tile("og23", [P, 2, NQ], F32)]
-        og_sb = [og_tiles[0][:, 0, :], og_tiles[1][:, 0, :], og_tiles[2][:, 0, :], og_tiles[2][:, 1, :]]
+        v_pool = [placed("v_pool%d" % t, [P, T], F32, 8192 * t) for t in range(PACK)]
+        res = tile("res", [P, PACK, NQ], F32)
+        og_tiles = [placed("og0", [P, 1, NQ], F32, 32768), res[:, 2:3, :], tile("og2", [P, 1, NQ], F32), tile("og3", [P, 1, NQ], F32)]
+        og_sb = [og_tile[:, 0, :] for og_tile in og_tiles]
         gates = [tile("gate%d" % t, [P, NQ], F32) for t in range(PACK)]
 
         q_rows = qT[0].rearrange("(g p t) q -> g p t q", p=P, t=PACK)
@@ -75,30 +82,31 @@ def tile_attend_plo_siggate_topk_kernel(tc, qT, k_words, k_scales, vT, th, og, u
         table_warm = tile("table_warm", [P, 1], F32)
         nc.scalar.activation(table_warm[64:128, :], th_rows[64:128, 0:1], SIGMOID)
 
-        th_ps = ps.tile([P, P], F32, name="th_ps", tag="vt", bufs=2)
+        th_ps = ps.tile([P, P], F32, name="th_ps", tag="vt", bufs=3)
         nc.tensor.transpose(th_ps[:], th_rows[:], ident[:])
         neg_th = tile("neg_th", [P, NQ // P], F32)
         nc.scalar.activation(neg_th[:], th_ps[:, 0 : NQ // P], COPY, scale=-1.0)
 
-        us_ps = ps.tile([P, PACK, P], F32, name="us_ps", tag="vt", bufs=2)
+        us_ps = ps.tile([P, PACK, P], F32, name="us_ps", tag="vt", bufs=3)
         for r in range(PACK):
             nc.tensor.transpose(us_ps[:, r, :], us_rows[:, r:N:PACK], ident[:])
         nc.scalar.copy(us_sb[:], us_ps[:, :, 0])
 
         ks_picked = tile("ks_picked", [P, N], U8)
         nc.vector.tensor_copy(ks_picked[:], ks_pool[:].indirect(offsets[:]))
+        nc.vector.tensor_copy(ks[0][0:32, :].bitcast(I32), ks_picked[0:32, :].bitcast(I32))
         for g in range(PASSES):
             nc.sync.dma_start(q_raw[g][:], q_rows[g])
-            for quad in range(4):
+            for quad in range(1 - g, 4):
                 row = 16 * g + 4 * quad
                 nc.sync.dma_start(
                     ks[g][32 * quad : 32 * quad + 4, :].bitcast(I32), ks_picked[row : row + 4, :].bitcast(I32)
                 )
+        og_rows = og[0].rearrange("(p t) q -> p t q", t=PACK)
         for t in range(PACK):
             nc.sync.dma_start(v_pool[t][:], v_rows[t])
-        og_rows = og[0].rearrange("(p t) q -> p t q", t=PACK)
-        for og_tile, rows in zip(og_tiles, (slice(0, 1), slice(1, 2), slice(2, 4))):
-            nc.sync.dma_start(og_tile[:], og_rows[:, rows, :])
+        for t in range(PACK):
+            nc.sync.dma_start(og_tiles[t][:, :, :], og_rows[:, t : t + 1, :])
         kw = tile("kw", [P, N], U32)
         nc.vector.tensor_copy(kw[:], kw_pool[:].bitcast(U32).indirect(offsets[:]))
         k_codes = [tile("k_codes%d" % g, [P, 2 * N], U8) for g in range(PASSES)]
@@ -130,29 +138,21 @@ def tile_attend_plo_siggate_topk_kernel(tc, qT, k_words, k_scales, vT, th, og, u
 
         halves = [slice(h * HALF, (h + 1) * HALF) for h in range(2)]
         v_turned = {}
+        v_picked = {}
         v_codes = {}
         v_scales = {}
 
         def v_turn(t, word_sets):
-            v_turned[t] = ps.tile([P, 2, P], F32, name="v_turned%d" % t, tag="vt", bufs=2)
+            v_turned[t] = ps.tile([P, 2, P], F32, name="v_turned%d" % t, tag="vt", bufs=3)
             for u in range(2):
                 nc.tensor.transpose(v_turned[t][:, u, :], word_sets[u], ident[:])
 
         def v_pick(t):
             picked = tile("v_picked%d" % t, [P, N], BF16)
+            v_picked[t] = picked
             nc.vector.tensor_copy(picked[:], v_pool[t][:].indirect(offsets[:]))
             words = picked[:].bitcast(F32)
             v_turn(t, [words[:, u : 2 * P : 2] for u in range(2)])
-
-        def v_pick_on_scalar(t):
-            rounded = tile("v_rounded%d" % t, [P, T], BF16)
-            nc.scalar.activation(rounded[:], v_pool[t][:], COPY)
-            picked = tile("v_picked%d" % t, [P, N], BF16)
-            nc.scalar.activation(
-                picked[:].rearrange("p (u s e) -> p s u e", u=2, e=2), rounded[:].indirect(offsets[:]), COPY
-            )
-            words = picked[:].bitcast(F32)
-            v_turn(t, [words[:, u * P : (u + 1) * P] for u in range(2)])
 
         def v_copy(t, grouped):
             nc.scalar.copy(
@@ -160,90 +160,119 @@ def tile_attend_plo_siggate_topk_kernel(tc, qT, k_words, k_scales, vT, th, og, u
                 v_turned[t][:].rearrange("p u c -> p c u"),
             )
 
-        def v_quant(first, grouped, count, tag=None):
-            codes = tile("v_codes%d" % first, [P, count * P], U32, tag=tag)
+        def v_quant(first, count, grouped, codes):
             scales = tile("v_scales%d" % first, [P, count * P], U8)
-            quantize(nc, codes[:], scales[:], grouped[:])
+            quantize(nc, codes[:], scales[:], grouped[:, :, :])
             for i in range(count):
                 v_codes[first + i] = codes[:, i * P : (i + 1) * P]
                 v_scales[first + i] = scales[:, i * P : (i + 1) * P]
 
-        y_codes = tile("y_codes", [P, NQ], U32)
-        y_scales = tile("y_scales", [P, NQ], U8)
+        y_codes = {}
+        y_scales = {}
 
-        def y_block(j):
+        def y_quant(h, codes):
+            y_codes[h] = codes
+            y_scales[h] = tile("y_scales%d" % h, [P, HALF], U8)
+            quantize(nc, codes[:], y_scales[h][:], y_grp[:, halves[h], :])
+
+        y_turned = {}
+
+        def y_scale_on_scalar(j, first):
+            for r in range(PACK):
+                nc.scalar.activation(
+                    y_grp[:, j * P + first : (j + 1) * P, r], y_turned[j][:, r, first:P], COPY, scale=us_sb[:, r : r + 1]
+                )
+
+        def y_block(j, cols=P):
             sig = tile("sig%d" % j, [P, PACK, P], F32)
             nc.scalar.activation(
                 sig[:], score[j][:].rearrange("p (s r) -> p r s", r=PACK), SIGMOID, bias=neg_th[:, j : j + 1]
             )
-            turned = ps.tile([P, PACK, P], F32, name="y_turned%d" % j, tag="yt", bufs=2)
+            turned = ps.tile([P, PACK, P], F32, name="y_turned%d" % j, tag="acc%d" % j)
             for r in range(PACK):
                 nc.tensor.transpose(turned[:, r, :], sig[:, r, :], ident[:])
-            nc.vector.tensor_tensor(
-                y_grp[:, j * P : (j + 1) * P, :],
-                turned[:].rearrange("p r q -> p q r"),
-                us_sb[:].unsqueeze(1).broadcast_to([P, P, PACK]),
-                MULT,
-            )
+            y_turned[j] = turned
+            if cols:
+                nc.vector.tensor_tensor(
+                    y_grp[:, j * P : j * P + cols, :],
+                    turned[:, :, 0:cols].rearrange("p r q -> p q r"),
+                    us_sb[:].unsqueeze(1).broadcast_to([P, cols, PACK]),
+                    MULT,
+                )
 
         def gate_tile(t):
             nc.scalar.activation(gates[t][:], og_sb[t], SIGMOID)
 
-        def product(acc, t, cols):
+        def product(acc, t, h):
             nc.tensor.matmul_mx(
                 acc,
                 lhsT=v_codes[t].bitcast(FP8X4),
                 lhsT_scale=v_scales[t],
-                rhs=y_codes[:, cols].bitcast(FP8X4),
-                rhs_scale=y_scales[:, cols],
+                rhs=y_codes[h][:].bitcast(FP8X4),
+                rhs_scale=y_scales[h][:],
                 start=True,
                 stop=True,
             )
 
-        v_pick(0)
-        y_grp = tile("y_grp", [P, NQ, PACK], BF16, tag="v_pool0")
-        for h in range(2):
-            y_block(2 * h)
-            y_block(2 * h + 1)
-            quantize(nc, y_codes[:, halves[h]], y_scales[:, halves[h]], y_grp[:, halves[h], :])
-        accs = [ps.tile([P, NQ], F32, name="o%d" % t, tag="acc%d" % t) for t in range(PACK - 1)]
-        v_grp0 = tile("v_grp0", [P, P, PACK], BF16)
-        v_copy(0, v_grp0[:])
-        v_quant(0, v_grp0, 1)
-        product(accs[0][:], 0, slice(0, NQ))
-        v_pick_on_scalar(1)
-        v_pick(2)
-        v_grp12 = tile("v_grp12", [P, 2 * P, PACK], BF16)
-        v_copy(1, v_grp12[:, 0:P, :])
-        v_copy(2, v_grp12[:, P : 2 * P, :])
-        v_pick(3)
-        v_quant(1, v_grp12, 2, tag="v_pool3")
-        gate_tile(0)
-        v_grp3 = tile("v_grp3", [P, P, PACK], BF16, tag="og0")
-        v_copy(3, v_grp3[:])
-        v_quant(3, v_grp3, 1)
-        gate_tile(1)
-        gate_tile(2)
-        gate_tile(3)
-
-        res = tile("res", [P, PACK, NQ], F32)
         out_rows = out_0.rearrange("(p t) q -> p t q", t=PACK)
-        for t in range(PACK):
-            gate = gates[t]
-            if t < PACK - 1:
-                acc = accs[t]
-                if t > 0:
-                    product(acc[:], t, slice(0, NQ))
-                nc.vector.tensor_tensor(res[:, t, :], acc[:], gate[:], MULT)
-            else:
-                first = ps.tile([P, HALF], F32, name="o_first", tag="acc%d" % t)
-                second = ps.tile([P, HALF], F32, name="o_second", tag="yt", bufs=2)
-                sums = [first[:], second[:]]
-                for h in range(2):
-                    product(sums[h], t, halves[h])
-                for h in range(2):
-                    nc.vector.tensor_tensor(res[:, t, halves[h]], sums[h], gate[:, halves[h]], MULT)
+
+        def gated(t, acc, cols):
+            nc.vector.tensor_tensor(res[:, t, cols], acc, gates[t][:, cols], MULT)
+
+        def store(t):
             nc.sync.dma_start(out_rows[:, t, :], res[:, t, :])
+
+        def products(t):
+            for h in range(2):
+                product(accs[t][:, halves[h]], t, h)
+
+        whole = slice(0, NQ)
+        v_pick(0)
+        y_grp = placed("y_grp", [P, NQ, PACK], BF16, 0)
+        y_block(0)
+        y_block(1)
+        y_block(2, 64)
+        y_quant(0, tile("y_codes0", [P, HALF], U32))
+        y_block(3, 0)
+        y_scale_on_scalar(3, 0)
+        y_scale_on_scalar(2, 64)
+        v_pick(1)
+        accs = [ps.tile([P, NQ], F32, name="o%d" % t, tag="acc%d" % t) for t in range(PACK - 1)]
+        v_grp01 = tile("v_grp01", [P, 2 * P, PACK], BF16)
+        v_copy(0, v_grp01[:, 0:P, :])
+        v_copy(1, v_grp01[:, P : 2 * P, :])
+        v_pick(2)
+        y_quant(1, placed("y_codes1", [P, HALF], U32, 16384))
+        v_quant(0, 2, v_grp01, placed("v_codes01", [P, 2 * P], U32, 17408))
+        products(0)
+        products(1)
+        v_grp2 = tile("v_grp2", [P, P, PACK], BF16)
+        v_copy(2, v_grp2[:])
+        v_pick(3)
+        gate_tile(0)
+        gate_tile(1)
+        v_quant(2, 1, v_grp2, placed("v_codes2", [P, P], U32, 32768))
+        products(2)
+        gated(0, accs[0][:], whole)
+        store(0)
+        gated(1, accs[1][:], whole)
+        store(1)
+        gate_tile(2)
+        v_grp3 = res[:, 2, halves[1]].bitcast(BF16).rearrange("p (c t) -> p c t", t=PACK)
+        v_copy(3, v_grp3)
+        gated(2, accs[2][:, halves[0]], halves[0])
+        v_quant(3, 1, v_grp3, tile("v_codes3", [P, P], U32))
+        gate_tile(3)
+        gated(2, accs[2][:, halves[1]], halves[1])
+        store(2)
+        first = ps.tile([P, HALF], F32, name="o_first", tag="acc3")
+        second = ps.tile([P, HALF], F32, name="o_second", tag="spare")
+        sums = [first[:], second[:]]
+        for h in range(2):
+            product(sums[h], 3, h)
+        for h in range(2):
+            gated(3, sums[h], halves[h])
+        store(3)
 
         o_scales = tile("o_scales", [P, NQ], U8)
         words_out = out_1[0].rearrange("p q b -> p (q b)").bitcast(I32)

@@ -21,7 +21,7 @@ D, T, N, NQ, DV = 1024, 2048, 512, 512, 512
 PASSES = D // (P * PACK)
 HALF = NQ // 2
 
-SCALAR_COLS = 192
+SCALAR_COLS = 144
 
 FLOPS = 2 * N * NQ * (D + DV)
 
@@ -113,23 +113,24 @@ def tile_attend_plo_siggate_topk_kernel(tc, qT, k_words, k_scales, vT, th, og, u
         for g in range(PASSES):
             nc.vector.tensor_copy(k_codes[g][:].bitcast(U16), kw[:].bitcast(U16)[:, g : 2 * N : 2])
 
-        q_codes = [[tile("q_codes%d%d" % (g, h), [P, HALF], U32) for h in range(2)] for g in range(PASSES)]
-        q_scales = [[tile("q_scales%d%d" % (g, h), [P, HALF], U8) for h in range(2)] for g in range(PASSES)]
+        blocks = NQ // P
+        q_codes = [[tile("q_codes%d%d" % (g, j), [P, P], U32) for j in range(blocks)] for g in range(PASSES)]
+        q_scales = [[tile("q_scales%d%d" % (g, j), [P, P], U8) for j in range(blocks)] for g in range(PASSES)]
         for g in range(PASSES):
-            q_grp = [tile("q_grp%d%d" % (g, h), [P, HALF, PACK], BF16) for h in range(2)]
-            for h, copy in enumerate((nc.vector.tensor_copy, nc.scalar.copy)):
-                interleave(copy, q_grp[h][:], q_raw[g][:, :, h * HALF : (h + 1) * HALF])
-            for h in range(2):
-                quantize(nc, q_codes[g][h][:], q_scales[g][h][:], q_grp[h][:])
+            q_grp = [tile("q_grp%d%d" % (g, j), [P, P, PACK], BF16) for j in range(blocks)]
+            for j in range(blocks):
+                copy = nc.vector.tensor_copy if j < 2 else nc.scalar.copy
+                interleave(copy, q_grp[j][:], q_raw[g][:, :, j * P : (j + 1) * P])
+            for j in range(blocks):
+                quantize(nc, q_codes[g][j][:], q_scales[g][j][:], q_grp[j][:])
 
-        score = [ps.tile([P, N], F32, name="score%d" % j, tag="acc%d" % j) for j in range(4)]
+        score = [ps.tile([P, N], F32, name="score%d" % j, tag="acc%d" % j) for j in range(blocks)]
         for g in range(PASSES):
-            for j in range(4):
-                h, c = divmod(j, 2)
+            for j in range(blocks):
                 nc.tensor.matmul_mx(
                     score[j][:],
-                    lhsT=q_codes[g][h][:, c * P : (c + 1) * P].bitcast(FP8X4),
-                    lhsT_scale=q_scales[g][h][:, c * P : (c + 1) * P],
+                    lhsT=q_codes[g][j][:].bitcast(FP8X4),
+                    lhsT_scale=q_scales[g][j][:],
                     rhs=k_codes[g][:].bitcast(FP4X4),
                     rhs_scale=ks[g][:],
                     start=(g == 0),
@@ -203,13 +204,13 @@ def tile_attend_plo_siggate_topk_kernel(tc, qT, k_words, k_scales, vT, th, og, u
         def gate_tile(t):
             nc.scalar.activation(gates[t][:], og_sb[t], SIGMOID)
 
-        def product(acc, t, h):
+        def product(acc, t, h, cols=slice(0, HALF)):
             nc.tensor.matmul_mx(
                 acc,
                 lhsT=v_codes[t].bitcast(FP8X4),
                 lhsT_scale=v_scales[t],
-                rhs=y_codes[h][:].bitcast(FP8X4),
-                rhs_scale=y_scales[h][:],
+                rhs=y_codes[h][:, cols].bitcast(FP8X4),
+                rhs_scale=y_scales[h][:, cols],
                 start=True,
                 stop=True,
             )
@@ -265,21 +266,23 @@ def tile_attend_plo_siggate_topk_kernel(tc, qT, k_words, k_scales, vT, th, og, u
         gate_tile(3)
         gated(2, accs[2][:, halves[1]], halves[1])
         store(2)
-        first = ps.tile([P, HALF], F32, name="o_first", tag="acc3")
-        second = ps.tile([P, HALF], F32, name="o_second", tag="spare")
-        sums = [first[:], second[:]]
-        for h in range(2):
-            product(sums[h], 3, h)
-        for h in range(2):
-            gated(3, sums[h], halves[h])
+        pieces = [(0, slice(0, P), "acc3", 1), (0, slice(P, HALF), "vt", 3), (1, slice(0, HALF), "spare", 1)]
+        sums = []
+        for i, (h, cols, bank, bufs) in enumerate(pieces):
+            sums.append(ps.tile([P, cols.stop - cols.start], F32, name="o3_%d" % i, tag=bank, bufs=bufs))
+            product(sums[i][:], 3, h, cols)
+        for i, (h, cols, bank, bufs) in enumerate(pieces):
+            gated(3, sums[i][:], slice(h * HALF + cols.start, h * HALF + cols.stop))
         store(3)
 
         o_scales = tile("o_scales", [P, NQ], U8)
         words_out = out_1[0].rearrange("p q b -> p (q b)").bitcast(I32)
         o_grp = [tile("o_grp%d" % h, [P, HALF, PACK], BF16) for h in range(2)]
-        interleave(nc.scalar.copy, o_grp[0][:, 0:SCALAR_COLS, :], res[:, :, 0:SCALAR_COLS])
-        interleave(nc.vector.tensor_copy, o_grp[0][:, SCALAR_COLS:HALF, :], res[:, :, SCALAR_COLS:HALF])
-        interleave(nc.vector.tensor_copy, o_grp[1][:], res[:, :, halves[1]])
+        for pair in (slice(0, 2), slice(2, 4)):
+            interleave(nc.scalar.copy, o_grp[0][:, 0:P, pair], res[:, pair, 0:P])
+            interleave(nc.scalar.copy, o_grp[1][:, 0:SCALAR_COLS, pair], res[:, pair, HALF : HALF + SCALAR_COLS])
+        interleave(nc.vector.tensor_copy, o_grp[0][:, P:HALF, :], res[:, :, P:HALF])
+        interleave(nc.vector.tensor_copy, o_grp[1][:, SCALAR_COLS:HALF, :], res[:, :, HALF + SCALAR_COLS : NQ])
         for h in range(2):
             o_codes = tile("o_codes%d" % h, [P, HALF], U32)
             quantize(nc, o_codes[:], o_scales[:, halves[h]], o_grp[h][:])

@@ -58,9 +58,7 @@ def tile_attend_plo_siggate_topk_kernel(tc, qT, k_words, k_scales, vT, th, og, u
         nc.vector.memset(ks[0][32:64, :].bitcast(I32), 0)
         nc.vector.memset(ks[0][64:128, :].bitcast(I32), 0)
         nc.vector.memset(ks[1][:].bitcast(I32), 0)
-        us_rows = tile("us_rows", [P, N], F32)
         nc.gpsimd.memset(th_rows[:], 0.0)
-        nc.gpsimd.memset(us_rows[:], 0.0)
         make_identity(nc, ident[:])
 
         q_raw = [tile("q_raw%d" % g, [P, PACK, NQ], F32) for g in range(PASSES)]
@@ -77,7 +75,6 @@ def tile_attend_plo_siggate_topk_kernel(tc, qT, k_words, k_scales, vT, th, og, u
         nc.sync.dma_start(ks_pool[0:32, :].bitcast(I32), k_scales.rearrange("o f t -> (o f) t").bitcast(I32))
         nc.sync.dma_start(kw_pool[:], k_words[0].rearrange("p t b -> p (t b)").bitcast(I32))
         nc.scalar.dma_start(th_rows[0:4, :], th[0, 0].rearrange("(j p) -> j p", p=P))
-        nc.scalar.dma_start(us_rows[0:1, :], us[0].rearrange("n one -> one n"))
         v_rows = vT.rearrange("(p t) n -> t p n", t=PACK)
         table_warm = tile("table_warm", [P, 1], F32)
         nc.scalar.activation(table_warm[64:128, :], th_rows[64:128, 0:1], SIGMOID)
@@ -86,11 +83,6 @@ def tile_attend_plo_siggate_topk_kernel(tc, qT, k_words, k_scales, vT, th, og, u
         nc.tensor.transpose(th_ps[:], th_rows[:], ident[:])
         neg_th = tile("neg_th", [P, NQ // P], F32)
         nc.scalar.activation(neg_th[:], th_ps[:, 0 : NQ // P], COPY, scale=-1.0)
-
-        us_ps = ps.tile([P, PACK, P], F32, name="us_ps", tag="vt", bufs=3)
-        for r in range(PACK):
-            nc.tensor.transpose(us_ps[:, r, :], us_rows[:, r:N:PACK], ident[:])
-        nc.scalar.copy(us_sb[:], us_ps[:, :, 0])
 
         ks_picked = tile("ks_picked", [P, N], U8)
         nc.vector.tensor_copy(ks_picked[:], ks_pool[:].indirect(offsets[:]))
@@ -105,6 +97,8 @@ def tile_attend_plo_siggate_topk_kernel(tc, qT, k_words, k_scales, vT, th, og, u
         og_rows = og[0].rearrange("(p t) q -> p t q", t=PACK)
         for t in range(PACK):
             nc.sync.dma_start(v_pool[t][:], v_rows[t])
+            if t == 0:
+                nc.sync.dma_start(us_sb[:], us[0].rearrange("(p r) one -> p (r one)", r=PACK))
         for t in range(PACK):
             nc.sync.dma_start(og_tiles[t][:, :, :], og_rows[:, t : t + 1, :])
         kw = tile("kw", [P, N], U32)
@@ -229,7 +223,7 @@ def tile_attend_plo_siggate_topk_kernel(tc, qT, k_words, k_scales, vT, th, og, u
 
         whole = slice(0, NQ)
         v_pick(0)
-        y_grp = placed("y_grp", [P, NQ, PACK], BF16, 0)
+        y_grp = tile("y_grp", [P, NQ, PACK], BF16)
         y_block(0)
         y_block(1)
         y_block(2, 64)

@@ -21,7 +21,8 @@ D, T, N, NQ, DV = 1024, 2048, 512, 512, 512
 PASSES = D // (P * PACK)
 HALF = NQ // 2
 
-SCALAR_COLS = 144
+SCALAR_COLS = 128
+GATE_AHEAD = 384
 
 FLOPS = 2 * N * NQ * (D + DV)
 
@@ -66,7 +67,7 @@ def tile_attend_plo_siggate_topk_kernel(tc, qT, k_words, k_scales, vT, th, og, u
         us_sb = tile("us_sb", [P, PACK], F32)
         v_pool = [placed("v_pool%d" % t, [P, T], F32, 8192 * t) for t in range(PACK)]
         res = tile("res", [P, PACK, NQ], F32)
-        og_tiles = [placed("og0", [P, 1, NQ], F32, 32768), res[:, 2:3, :], tile("og2", [P, 1, NQ], F32), tile("og3", [P, 1, NQ], F32)]
+        og_tiles = [placed("og0", [P, 1, NQ], F32, 32768), placed("og1", [P, 1, NQ], F32, 34816), tile("og2", [P, 1, NQ], F32), tile("og3", [P, 1, NQ], F32)]
         og_sb = [og_tile[:, 0, :] for og_tile in og_tiles]
         gates = [tile("gate%d" % t, [P, NQ], F32) for t in range(PACK)]
 
@@ -173,10 +174,10 @@ def tile_attend_plo_siggate_topk_kernel(tc, qT, k_words, k_scales, vT, th, og, u
         y_turned = {}
 
         def y_scale_on_scalar(j, first):
+            staged = tile("y_staged%d" % j, [P, PACK, P - first], BF16)
             for r in range(PACK):
-                nc.scalar.activation(
-                    y_grp[:, j * P + first : (j + 1) * P, r], y_turned[j][:, r, first:P], COPY, scale=us_sb[:, r : r + 1]
-                )
+                nc.scalar.activation(staged[:, r, :], y_turned[j][:, r, first:P], COPY, scale=us_sb[:, r : r + 1])
+            interleave(nc.scalar.copy, y_grp[:, j * P + first : (j + 1) * P, :], staged[:])
 
         def y_block(j, cols=P):
             sig = tile("sig%d" % j, [P, PACK, P], F32)
@@ -195,8 +196,8 @@ def tile_attend_plo_siggate_topk_kernel(tc, qT, k_words, k_scales, vT, th, og, u
                     MULT,
                 )
 
-        def gate_tile(t):
-            nc.scalar.activation(gates[t][:], og_sb[t], SIGMOID)
+        def gate_tile(t, cols=slice(0, NQ)):
+            nc.scalar.activation(gates[t][:, cols], og_sb[t][:, cols], SIGMOID)
 
         def product(acc, t, h, cols=slice(0, HALF)):
             nc.tensor.matmul_mx(
@@ -226,11 +227,15 @@ def tile_attend_plo_siggate_topk_kernel(tc, qT, k_words, k_scales, vT, th, og, u
         y_grp = tile("y_grp", [P, NQ, PACK], BF16)
         y_block(0)
         y_block(1)
-        y_block(2, 64)
-        y_quant(0, tile("y_codes0", [P, HALF], U32))
+        y_codes[0] = tile("y_codes0", [P, HALF], U32)
+        y_scales[0] = tile("y_scales0", [P, HALF], U8)
+        for j in range(2):
+            cols = slice(j * P, (j + 1) * P)
+            quantize(nc, y_codes[0][:, cols], y_scales[0][:, cols], y_grp[:, cols, :])
+        y_block(2, 0)
         y_block(3, 0)
+        y_scale_on_scalar(2, 0)
         y_scale_on_scalar(3, 0)
-        y_scale_on_scalar(2, 64)
         v_pick(1)
         accs = [ps.tile([P, NQ], F32, name="o%d" % t, tag="acc%d" % t) for t in range(PACK - 1)]
         v_grp01 = tile("v_grp01", [P, 2 * P, PACK], BF16)
@@ -252,13 +257,13 @@ def tile_attend_plo_siggate_topk_kernel(tc, qT, k_words, k_scales, vT, th, og, u
         store(0)
         gated(1, accs[1][:], whole)
         store(1)
-        gate_tile(2)
-        v_grp3 = res[:, 2, halves[1]].bitcast(BF16).rearrange("p (c t) -> p c t", t=PACK)
-        v_copy(3, v_grp3)
-        gated(2, accs[2][:, halves[0]], halves[0])
+        gate_tile(2, slice(0, GATE_AHEAD))
+        v_grp3 = placed("v_grp3", [P, P, PACK], BF16, 34816)
+        v_copy(3, v_grp3[:])
+        gate_tile(2, slice(GATE_AHEAD, NQ))
         v_quant(3, 1, v_grp3, tile("v_codes3", [P, P], U32))
         gate_tile(3)
-        gated(2, accs[2][:, halves[1]], halves[1])
+        gated(2, accs[2][:], whole)
         store(2)
         pieces = [(0, slice(0, P), "acc3", 1), (0, slice(P, HALF), "vt", 3), (1, slice(0, HALF), "spare", 1)]
         sums = []

@@ -21,7 +21,7 @@ D, T, N, NQ, DV = 1024, 2048, 512, 512, 512
 PASSES = D // (P * PACK)
 HALF = NQ // 2
 
-SCALAR_COLS = 128
+SCALAR_COLS = 112
 GATE_AHEAD = 384
 
 FLOPS = 2 * N * NQ * (D + DV)
@@ -73,7 +73,7 @@ def tile_attend_plo_siggate_topk_kernel(tc, qT, k_words, k_scales, vT, th, og, u
 
         q_rows = qT[0].rearrange("(g p t) q -> g p t q", p=P, t=PACK)
         nc.sync.dma_start(offsets[:], offs)
-        nc.sync.dma_start(ks_pool[0:32, :].bitcast(I32), k_scales.rearrange("o f t -> (o f) t").bitcast(I32))
+        nc.scalar.dma_start(ks_pool[0:32, :].bitcast(I32), k_scales.rearrange("o f t -> (o f) t").bitcast(I32))
         nc.sync.dma_start(kw_pool[:], k_words[0].rearrange("p t b -> p (t b)").bitcast(I32))
         nc.scalar.dma_start(th_rows[0:4, :], th[0, 0].rearrange("(j p) -> j p", p=P))
         v_rows = vT.rearrange("(p t) n -> t p n", t=PACK)
@@ -262,7 +262,8 @@ def tile_attend_plo_siggate_topk_kernel(tc, qT, k_words, k_scales, vT, th, og, u
         v_copy(3, v_grp3[:])
         gate_tile(2, slice(GATE_AHEAD, NQ))
         v_quant(3, 1, v_grp3, tile("v_codes3", [P, P], U32))
-        gate_tile(3)
+        gate_tile(3, halves[0])
+        gate_tile(3, halves[1])
         gated(2, accs[2][:], whole)
         store(2)
         pieces = [(0, slice(0, P), "acc3", 1), (0, slice(P, HALF), "vt", 3), (1, slice(0, HALF), "spare", 1)]
@@ -279,7 +280,7 @@ def tile_attend_plo_siggate_topk_kernel(tc, qT, k_words, k_scales, vT, th, og, u
         o_grp = [tile("o_grp%d" % h, [P, HALF, PACK], BF16) for h in range(2)]
         for pair in (slice(0, 2), slice(2, 4)):
             interleave(nc.scalar.copy, o_grp[0][:, 0:P, pair], res[:, pair, 0:P])
-            interleave(nc.scalar.copy, o_grp[1][:, 0:SCALAR_COLS, pair], res[:, pair, HALF : HALF + SCALAR_COLS])
+        interleave(nc.scalar.copy, o_grp[1][:, 0:SCALAR_COLS, :], res[:, :, HALF : HALF + SCALAR_COLS])
         interleave(nc.vector.tensor_copy, o_grp[0][:, P:HALF, :], res[:, :, P:HALF])
         interleave(nc.vector.tensor_copy, o_grp[1][:, SCALAR_COLS:HALF, :], res[:, :, HALF + SCALAR_COLS : NQ])
         for h in range(2):

@@ -21,7 +21,7 @@ D, T, N, NQ, DV = 1024, 2048, 512, 512, 512
 PASSES = D // (P * PACK)
 HALF = NQ // 2
 
-SCALAR_COLS = 112
+SCALAR_COLS = 96
 GATE_AHEAD = 384
 
 FLOPS = 2 * N * NQ * (D + DV)
@@ -73,7 +73,7 @@ def tile_attend_plo_siggate_topk_kernel(tc, qT, k_words, k_scales, vT, th, og, u
 
         q_rows = qT[0].rearrange("(g p t) q -> g p t q", p=P, t=PACK)
         nc.sync.dma_start(offsets[:], offs)
-        nc.scalar.dma_start(ks_pool[0:32, :].bitcast(I32), k_scales.rearrange("o f t -> (o f) t").bitcast(I32))
+        nc.sync.dma_start(ks_pool[0:32, :].bitcast(I32), k_scales.rearrange("o f t -> (o f) t").bitcast(I32))
         nc.sync.dma_start(kw_pool[:], k_words[0].rearrange("p t b -> p (t b)").bitcast(I32))
         nc.scalar.dma_start(th_rows[0:4, :], th[0, 0].rearrange("(j p) -> j p", p=P))
         v_rows = vT.rearrange("(p t) n -> t p n", t=PACK)
@@ -146,9 +146,11 @@ def tile_attend_plo_siggate_topk_kernel(tc, qT, k_words, k_scales, vT, th, og, u
         def v_pick(t):
             picked = tile("v_picked%d" % t, [P, N], BF16)
             v_picked[t] = picked
-            nc.vector.tensor_copy(picked[:], v_pool[t][:].indirect(offsets[:]))
+            nc.vector.tensor_copy(
+                picked[:].rearrange("p (u s e) -> p s u e", u=2, e=2), v_pool[t][:].indirect(offsets[:])
+            )
             words = picked[:].bitcast(F32)
-            v_turn(t, [words[:, u : 2 * P : 2] for u in range(2)])
+            v_turn(t, [words[:, u * P : (u + 1) * P] for u in range(2)])
 
         def v_copy(t, grouped):
             nc.scalar.copy(

@@ -229,14 +229,10 @@ def tile_attend_plo_siggate_topk_kernel(tc, qT, k_words, k_scales, vT, th, og, u
         y_grp = tile("y_grp", [P, NQ, PACK], BF16)
         y_block(0)
         y_block(1)
-        y_codes[0] = tile("y_codes0", [P, HALF], U32)
-        y_scales[0] = tile("y_scales0", [P, HALF], U8)
-        for j in range(2):
-            cols = slice(j * P, (j + 1) * P)
-            quantize(nc, y_codes[0][:, cols], y_scales[0][:, cols], y_grp[:, cols, :])
-        y_block(2, 0)
+        y_block(2, 64)
+        y_quant(0, tile("y_codes0", [P, HALF], U32))
         y_block(3, 0)
-        y_scale_on_scalar(2, 0)
+        y_scale_on_scalar(2, 64)
         y_scale_on_scalar(3, 0)
         v_pick(1)
         accs = [ps.tile([P, NQ], F32, name="o%d" % t, tag="acc%d" % t) for t in range(PACK - 1)]

@@ -17,12 +17,21 @@ SIGMOID = mybir.ActivationFunctionType.Sigmoid
 
 P = 128
 PACK = 4
+QUADS = 4
 D, T, N, NQ, DV = 1024, 2048, 512, 512, 512
 PASSES = D // (P * PACK)
+BANDS = NQ // P
 HALF = NQ // 2
 
-SCALAR_COLS = 96
-GATE_AHEAD = 384
+BAND2_ON_VECTOR = 64
+GATE2_AHEAD = 384
+GROUP_ON_SCALAR = 96
+
+POOL_BYTES = T * 4
+GATE_BYTES = NQ * 4
+ON_POOL2 = 2 * POOL_BYTES
+ON_GATE0 = PACK * POOL_BYTES
+ON_GATE1 = ON_GATE0 + GATE_BYTES
 
 FLOPS = 2 * N * NQ * (D + DV)
 
@@ -40,88 +49,101 @@ def tile_attend_plo_siggate_topk_kernel(tc, qT, k_words, k_scales, vT, th, og, u
     with ExitStack() as ctx:
         sb = ctx.enter_context(tc.tile_pool(name="sb", bufs=1))
         ps = ctx.enter_context(tc.psum_pool(name="ps", bufs=1))
-
         shared = ctx.enter_context(tc.tile_pool(name="shared", bufs=1))
 
-        def tile(name, shape, dtype, tag=None):
-            return sb.tile(shape, dtype, name=name, tag=tag or name, align_bytes=64)
+        def tile(name, shape, dtype):
+            return sb.tile(shape, dtype, name=name, tag=name, align_bytes=64)
 
         def placed(name, shape, dtype, offset):
             return shared.tile(shape, dtype, name=name, tag=name, align_bytes=64, offset=offset)
+
+        def turn_bank(name, shape):
+            return ps.tile(shape, F32, name=name, tag="turn", bufs=3)
+
+        halves = [slice(h * HALF, (h + 1) * HALF) for h in range(2)]
+        whole = slice(0, NQ)
 
         offsets = tile("offsets", [P, N // 16], U16)
         ks_pool = tile("ks_pool", [P, T], U8)
         ks = [tile("ks%d" % g, [P, N], U8) for g in range(PASSES)]
         th_rows = tile("th_rows", [P, P], F32)
         ident = tile("ident", [P, P], F32)
+        warm_in = tile("warm_in", [P, 1], F32)
         nc.vector.memset(ks_pool[32:64, :].bitcast(I32), 0)
         nc.vector.memset(ks_pool[64:128, :].bitcast(I32), 0)
         nc.vector.memset(ks[0][32:64, :].bitcast(I32), 0)
         nc.vector.memset(ks[0][64:128, :].bitcast(I32), 0)
         nc.vector.memset(ks[1][:].bitcast(I32), 0)
         nc.gpsimd.memset(th_rows[:], 0.0)
+        nc.gpsimd.memset(warm_in[:], 0.0)
         make_identity(nc, ident[:])
 
         q_raw = [tile("q_raw%d" % g, [P, PACK, NQ], F32) for g in range(PASSES)]
         kw_pool = tile("kw_pool", [P, T], I32)
         us_sb = tile("us_sb", [P, PACK], F32)
-        v_pool = [placed("v_pool%d" % t, [P, T], F32, 8192 * t) for t in range(PACK)]
+        v_pool = [placed("v_pool%d" % t, [P, T], F32, POOL_BYTES * t) for t in range(PACK)]
         res = tile("res", [P, PACK, NQ], F32)
-        og_tiles = [placed("og0", [P, 1, NQ], F32, 32768), placed("og1", [P, 1, NQ], F32, 34816), tile("og2", [P, 1, NQ], F32), tile("og3", [P, 1, NQ], F32)]
-        og_sb = [og_tile[:, 0, :] for og_tile in og_tiles]
+        og_sb = [
+            placed("og0", [P, 1, NQ], F32, ON_GATE0),
+            placed("og1", [P, 1, NQ], F32, ON_GATE1),
+            tile("og2", [P, 1, NQ], F32),
+            tile("og3", [P, 1, NQ], F32),
+        ]
         gates = [tile("gate%d" % t, [P, NQ], F32) for t in range(PACK)]
 
-        q_rows = qT[0].rearrange("(g p t) q -> g p t q", p=P, t=PACK)
         nc.sync.dma_start(offsets[:], offs)
         nc.sync.dma_start(ks_pool[0:32, :].bitcast(I32), k_scales.rearrange("o f t -> (o f) t").bitcast(I32))
         nc.sync.dma_start(kw_pool[:], k_words[0].rearrange("p t b -> p (t b)").bitcast(I32))
-        nc.scalar.dma_start(th_rows[0:4, :], th[0, 0].rearrange("(j p) -> j p", p=P))
-        v_rows = vT.rearrange("(p t) n -> t p n", t=PACK)
-        table_warm = tile("table_warm", [P, 1], F32)
-        nc.scalar.activation(table_warm[64:128, :], th_rows[64:128, 0:1], SIGMOID)
+        nc.scalar.dma_start(th_rows[0:BANDS, :], th[0, 0].rearrange("(j p) -> j p", p=P))
 
-        th_ps = ps.tile([P, P], F32, name="th_ps", tag="vt", bufs=3)
+        warm_out = tile("warm_out", [P, 1], F32)
+        nc.scalar.activation(warm_out[:], warm_in[:], SIGMOID)
+
+        th_ps = turn_bank("th_ps", [P, P])
         nc.tensor.transpose(th_ps[:], th_rows[:], ident[:])
-        neg_th = tile("neg_th", [P, NQ // P], F32)
-        nc.scalar.activation(neg_th[:], th_ps[:, 0 : NQ // P], COPY, scale=-1.0)
+        neg_th = tile("neg_th", [P, BANDS], F32)
+        nc.scalar.activation(neg_th[:], th_ps[:, 0:BANDS], COPY, scale=-1.0)
 
         ks_picked = tile("ks_picked", [P, N], U8)
         nc.vector.tensor_copy(ks_picked[:], ks_pool[:].indirect(offsets[:]))
         nc.vector.tensor_copy(ks[0][0:32, :].bitcast(I32), ks_picked[0:32, :].bitcast(I32))
+        q_rows = qT[0].rearrange("(g p t) q -> g p t q", p=P, t=PACK)
         for g in range(PASSES):
             nc.sync.dma_start(q_raw[g][:], q_rows[g])
-            for quad in range(1 - g, 4):
+            for quad in range(1 - g, QUADS):
                 row = 16 * g + 4 * quad
                 nc.sync.dma_start(
                     ks[g][32 * quad : 32 * quad + 4, :].bitcast(I32), ks_picked[row : row + 4, :].bitcast(I32)
                 )
+
+        v_rows = vT.rearrange("(p t) n -> t p n", t=PACK)
         og_rows = og[0].rearrange("(p t) q -> p t q", t=PACK)
-        for t in range(PACK):
+        nc.sync.dma_start(v_pool[0][:], v_rows[0])
+        nc.sync.dma_start(us_sb[:], us[0].rearrange("(p r) one -> p (r one)", r=PACK))
+        for t in range(1, PACK):
             nc.sync.dma_start(v_pool[t][:], v_rows[t])
-            if t == 0:
-                nc.sync.dma_start(us_sb[:], us[0].rearrange("(p r) one -> p (r one)", r=PACK))
         for t in range(PACK):
-            nc.sync.dma_start(og_tiles[t][:, :, :], og_rows[:, t : t + 1, :])
+            nc.sync.dma_start(og_sb[t][:], og_rows[:, t : t + 1, :])
+
         kw = tile("kw", [P, N], U32)
         nc.vector.tensor_copy(kw[:], kw_pool[:].bitcast(U32).indirect(offsets[:]))
         k_codes = [tile("k_codes%d" % g, [P, 2 * N], U8) for g in range(PASSES)]
         for g in range(PASSES):
             nc.vector.tensor_copy(k_codes[g][:].bitcast(U16), kw[:].bitcast(U16)[:, g : 2 * N : 2])
 
-        blocks = NQ // P
-        q_codes = [[tile("q_codes%d%d" % (g, j), [P, P], U32) for j in range(blocks)] for g in range(PASSES)]
-        q_scales = [[tile("q_scales%d%d" % (g, j), [P, P], U8) for j in range(blocks)] for g in range(PASSES)]
+        q_codes = [[tile("q_codes%d%d" % (g, j), [P, P], U32) for j in range(BANDS)] for g in range(PASSES)]
+        q_scales = [[tile("q_scales%d%d" % (g, j), [P, P], U8) for j in range(BANDS)] for g in range(PASSES)]
         for g in range(PASSES):
-            q_grp = [tile("q_grp%d%d" % (g, j), [P, P, PACK], BF16) for j in range(blocks)]
-            for j in range(blocks):
-                copy = nc.vector.tensor_copy if j < 2 else nc.scalar.copy
+            q_grp = [tile("q_grp%d%d" % (g, j), [P, P, PACK], BF16) for j in range(BANDS)]
+            for j in range(BANDS):
+                copy = nc.vector.tensor_copy if j < BANDS // 2 else nc.scalar.copy
                 interleave(copy, q_grp[j][:], q_raw[g][:, :, j * P : (j + 1) * P])
-            for j in range(blocks):
+            for j in range(BANDS):
                 quantize(nc, q_codes[g][j][:], q_scales[g][j][:], q_grp[j][:])
 
-        score = [ps.tile([P, N], F32, name="score%d" % j, tag="acc%d" % j) for j in range(blocks)]
+        score = [ps.tile([P, N], F32, name="score%d" % j, tag="acc%d" % j) for j in range(BANDS)]
         for g in range(PASSES):
-            for j in range(blocks):
+            for j in range(BANDS):
                 nc.tensor.matmul_mx(
                     score[j][:],
                     lhsT=q_codes[g][j][:].bitcast(FP8X4),
@@ -132,25 +154,19 @@ def tile_attend_plo_siggate_topk_kernel(tc, qT, k_words, k_scales, vT, th, og, u
                     stop=(g == PASSES - 1),
                 )
 
-        halves = [slice(h * HALF, (h + 1) * HALF) for h in range(2)]
         v_turned = {}
-        v_picked = {}
         v_codes = {}
         v_scales = {}
 
-        def v_turn(t, word_sets):
-            v_turned[t] = ps.tile([P, 2, P], F32, name="v_turned%d" % t, tag="vt", bufs=3)
-            for u in range(2):
-                nc.tensor.transpose(v_turned[t][:, u, :], word_sets[u], ident[:])
-
         def v_pick(t):
             picked = tile("v_picked%d" % t, [P, N], BF16)
-            v_picked[t] = picked
             nc.vector.tensor_copy(
                 picked[:].rearrange("p (u s e) -> p s u e", u=2, e=2), v_pool[t][:].indirect(offsets[:])
             )
             words = picked[:].bitcast(F32)
-            v_turn(t, [words[:, u * P : (u + 1) * P] for u in range(2)])
+            v_turned[t] = turn_bank("v_turned%d" % t, [P, 2, P])
+            for u in range(2):
+                nc.tensor.transpose(v_turned[t][:, u, :], words[:, u * P : (u + 1) * P], ident[:])
 
         def v_copy(t, grouped):
             nc.scalar.copy(
@@ -160,20 +176,32 @@ def tile_attend_plo_siggate_topk_kernel(tc, qT, k_words, k_scales, vT, th, og, u
 
         def v_quant(first, count, grouped, codes):
             scales = tile("v_scales%d" % first, [P, count * P], U8)
-            quantize(nc, codes[:], scales[:], grouped[:, :, :])
+            quantize(nc, codes[:], scales[:], grouped[:])
             for i in range(count):
                 v_codes[first + i] = codes[:, i * P : (i + 1) * P]
                 v_scales[first + i] = scales[:, i * P : (i + 1) * P]
 
+        y_grp = tile("y_grp", [P, NQ, PACK], BF16)
+        y_turned = {}
         y_codes = {}
         y_scales = {}
 
-        def y_quant(h, codes):
-            y_codes[h] = codes
-            y_scales[h] = tile("y_scales%d" % h, [P, HALF], U8)
-            quantize(nc, codes[:], y_scales[h][:], y_grp[:, halves[h], :])
+        def y_turn(j):
+            sig = tile("sig%d" % j, [P, PACK, P], F32)
+            nc.scalar.activation(
+                sig[:], score[j][:].rearrange("p (s r) -> p r s", r=PACK), SIGMOID, bias=neg_th[:, j : j + 1]
+            )
+            y_turned[j] = ps.tile([P, PACK, P], F32, name="y_turned%d" % j, tag="acc%d" % j)
+            for r in range(PACK):
+                nc.tensor.transpose(y_turned[j][:, r, :], sig[:, r, :], ident[:])
 
-        y_turned = {}
+        def y_scale_on_vector(j, last):
+            nc.vector.tensor_tensor(
+                y_grp[:, j * P : j * P + last, :],
+                y_turned[j][:, :, 0:last].rearrange("p r q -> p q r"),
+                us_sb[:].unsqueeze(1).broadcast_to([P, last, PACK]),
+                MULT,
+            )
 
         def y_scale_on_scalar(j, first):
             staged = tile("y_staged%d" % j, [P, PACK, P - first], BF16)
@@ -181,27 +209,15 @@ def tile_attend_plo_siggate_topk_kernel(tc, qT, k_words, k_scales, vT, th, og, u
                 nc.scalar.activation(staged[:, r, :], y_turned[j][:, r, first:P], COPY, scale=us_sb[:, r : r + 1])
             interleave(nc.scalar.copy, y_grp[:, j * P + first : (j + 1) * P, :], staged[:])
 
-        def y_block(j, cols=P):
-            sig = tile("sig%d" % j, [P, PACK, P], F32)
-            nc.scalar.activation(
-                sig[:], score[j][:].rearrange("p (s r) -> p r s", r=PACK), SIGMOID, bias=neg_th[:, j : j + 1]
-            )
-            turned = ps.tile([P, PACK, P], F32, name="y_turned%d" % j, tag="acc%d" % j)
-            for r in range(PACK):
-                nc.tensor.transpose(turned[:, r, :], sig[:, r, :], ident[:])
-            y_turned[j] = turned
-            if cols:
-                nc.vector.tensor_tensor(
-                    y_grp[:, j * P : j * P + cols, :],
-                    turned[:, :, 0:cols].rearrange("p r q -> p q r"),
-                    us_sb[:].unsqueeze(1).broadcast_to([P, cols, PACK]),
-                    MULT,
-                )
+        def y_quant(h, codes):
+            y_codes[h] = codes
+            y_scales[h] = tile("y_scales%d" % h, [P, HALF], U8)
+            quantize(nc, codes[:], y_scales[h][:], y_grp[:, halves[h], :])
 
-        def gate_tile(t, cols=slice(0, NQ)):
-            nc.scalar.activation(gates[t][:, cols], og_sb[t][:, cols], SIGMOID)
+        def gate_sigmoid(t, cols):
+            nc.scalar.activation(gates[t][:, cols], og_sb[t][:, 0, cols], SIGMOID)
 
-        def product(acc, t, h, cols=slice(0, HALF)):
+        def product(acc, t, h, cols):
             nc.tensor.matmul_mx(
                 acc,
                 lhsT=v_codes[t].bitcast(FP8X4),
@@ -212,65 +228,71 @@ def tile_attend_plo_siggate_topk_kernel(tc, qT, k_words, k_scales, vT, th, og, u
                 stop=True,
             )
 
-        out_rows = out_0.rearrange("(p t) q -> p t q", t=PACK)
+        def products(t):
+            for h in range(2):
+                product(accs[t][:, halves[h]], t, h, slice(0, HALF))
 
         def gated(t, acc, cols):
             nc.vector.tensor_tensor(res[:, t, cols], acc, gates[t][:, cols], MULT)
 
+        out_rows = out_0.rearrange("(p t) q -> p t q", t=PACK)
+
         def store(t):
             nc.sync.dma_start(out_rows[:, t, :], res[:, t, :])
 
-        def products(t):
-            for h in range(2):
-                product(accs[t][:, halves[h]], t, h)
-
-        whole = slice(0, NQ)
         v_pick(0)
-        y_grp = tile("y_grp", [P, NQ, PACK], BF16)
-        y_block(0)
-        y_block(1)
-        y_block(2, 64)
+        for j in range(2):
+            y_turn(j)
+            y_scale_on_vector(j, P)
+        y_turn(2)
+        y_scale_on_vector(2, BAND2_ON_VECTOR)
         y_quant(0, tile("y_codes0", [P, HALF], U32))
-        y_block(3, 0)
-        y_scale_on_scalar(2, 64)
+        y_turn(3)
+        y_scale_on_scalar(2, BAND2_ON_VECTOR)
         y_scale_on_scalar(3, 0)
         v_pick(1)
         accs = [ps.tile([P, NQ], F32, name="o%d" % t, tag="acc%d" % t) for t in range(PACK - 1)]
         v_grp01 = tile("v_grp01", [P, 2 * P, PACK], BF16)
         v_copy(0, v_grp01[:, 0:P, :])
         v_copy(1, v_grp01[:, P : 2 * P, :])
+
         v_pick(2)
-        y_quant(1, placed("y_codes1", [P, HALF], U32, 16384))
-        v_quant(0, 2, v_grp01, placed("v_codes01", [P, 2 * P], U32, 17408))
+        y_quant(1, placed("y_codes1", [P, HALF], U32, ON_POOL2))
+        v_quant(0, 2, v_grp01, placed("v_codes01", [P, 2 * P], U32, ON_POOL2 + HALF * 4))
         products(0)
         products(1)
         v_grp2 = tile("v_grp2", [P, P, PACK], BF16)
         v_copy(2, v_grp2[:])
+
         v_pick(3)
-        gate_tile(0)
-        gate_tile(1)
-        v_quant(2, 1, v_grp2, placed("v_codes2", [P, P], U32, 32768))
+        gate_sigmoid(0, whole)
+        gate_sigmoid(1, whole)
+        v_quant(2, 1, v_grp2, placed("v_codes2", [P, P], U32, ON_GATE0))
         products(2)
-        gated(0, accs[0][:], whole)
-        store(0)
-        gated(1, accs[1][:], whole)
-        store(1)
-        gate_tile(2, slice(0, GATE_AHEAD))
-        v_grp3 = placed("v_grp3", [P, P, PACK], BF16, 34816)
+        for t in range(2):
+            gated(t, accs[t][:], whole)
+            store(t)
+
+        gate_sigmoid(2, slice(0, GATE2_AHEAD))
+        v_grp3 = placed("v_grp3", [P, P, PACK], BF16, ON_GATE1)
         v_copy(3, v_grp3[:])
-        gate_tile(2, slice(GATE_AHEAD, NQ))
+        gate_sigmoid(2, slice(GATE2_AHEAD, NQ))
         v_quant(3, 1, v_grp3, tile("v_codes3", [P, P], U32))
-        gate_tile(3, halves[0])
-        gate_tile(3, halves[1])
+        for cols in halves:
+            gate_sigmoid(3, cols)
         gated(2, accs[2][:], whole)
         store(2)
-        pieces = [(0, slice(0, P), "acc3", 1), (0, slice(P, HALF), "vt", 3), (1, slice(0, HALF), "spare", 1)]
+
+        pieces = [(0, slice(0, P)), (0, slice(P, HALF)), (1, slice(0, HALF))]
         sums = []
-        for i, (h, cols, bank, bufs) in enumerate(pieces):
-            sums.append(ps.tile([P, cols.stop - cols.start], F32, name="o3_%d" % i, tag=bank, bufs=bufs))
-            product(sums[i][:], 3, h, cols)
-        for i, (h, cols, bank, bufs) in enumerate(pieces):
-            gated(3, sums[i][:], slice(h * HALF + cols.start, h * HALF + cols.stop))
+        sums.append(ps.tile([P, P], F32, name="o3_0", tag="acc3"))
+        product(sums[0][:], 3, *pieces[0])
+        sums.append(turn_bank("o3_1", [P, P]))
+        product(sums[1][:], 3, *pieces[1])
+        sums.append(ps.tile([P, HALF], F32, name="o3_2", tag="spare"))
+        product(sums[2][:], 3, *pieces[2])
+        for acc, (h, cols) in zip(sums, pieces):
+            gated(3, acc[:], slice(h * HALF + cols.start, h * HALF + cols.stop))
         store(3)
 
         o_scales = tile("o_scales", [P, NQ], U8)
@@ -278,14 +300,15 @@ def tile_attend_plo_siggate_topk_kernel(tc, qT, k_words, k_scales, vT, th, og, u
         o_grp = [tile("o_grp%d" % h, [P, HALF, PACK], BF16) for h in range(2)]
         for pair in (slice(0, 2), slice(2, 4)):
             interleave(nc.scalar.copy, o_grp[0][:, 0:P, pair], res[:, pair, 0:P])
-        interleave(nc.scalar.copy, o_grp[1][:, 0:SCALAR_COLS, :], res[:, :, HALF : HALF + SCALAR_COLS])
+        split = HALF + GROUP_ON_SCALAR
+        interleave(nc.scalar.copy, o_grp[1][:, 0:GROUP_ON_SCALAR, :], res[:, :, HALF:split])
         interleave(nc.vector.tensor_copy, o_grp[0][:, P:HALF, :], res[:, :, P:HALF])
-        interleave(nc.vector.tensor_copy, o_grp[1][:, SCALAR_COLS:HALF, :], res[:, :, HALF + SCALAR_COLS : NQ])
+        interleave(nc.vector.tensor_copy, o_grp[1][:, GROUP_ON_SCALAR:HALF, :], res[:, :, split:NQ])
         for h in range(2):
             o_codes = tile("o_codes%d" % h, [P, HALF], U32)
             quantize(nc, o_codes[:], o_scales[:, halves[h]], o_grp[h][:])
             nc.sync.dma_start(words_out[:, halves[h]], o_codes[:].bitcast(I32))
-        for quad in range(4):
+        for quad in range(QUADS):
             queue = nc.scalar if quad % 2 == 0 else nc.sync
             queue.dma_start(
                 out_2[0, 4 * quad : 4 * quad + 4, :].bitcast(I32),

from contextlib import ExitStack

import concourse.mybir as mybir
from concourse.masks import make_identity

F32 = mybir.dt.float32
BF16 = mybir.dt.bfloat16
I32 = mybir.dt.int32
U32 = mybir.dt.uint32
U16 = mybir.dt.uint16
U8 = mybir.dt.uint8
FP8X4 = mybir.dt.float8_e4m3fn_x4
FP4X4 = mybir.dt.float4_e2m1fn_x4
MULT = mybir.AluOpType.mult
COPY = mybir.ActivationFunctionType.Copy
SIGMOID = mybir.ActivationFunctionType.Sigmoid

P = 128
PACK = 4
QUADS = 4
D, T, N, NQ, DV = 1024, 2048, 512, 512, 512
PASSES = D // (P * PACK)
BANDS = NQ // P
HALF = NQ // 2

BAND2_ON_VECTOR = 64
GATE2_AHEAD = 384
GROUP_ON_SCALAR = 96

POOL_BYTES = T * 4
GATE_BYTES = NQ * 4
ON_POOL2 = 2 * POOL_BYTES
ON_GATE0 = PACK * POOL_BYTES
ON_GATE1 = ON_GATE0 + GATE_BYTES

FLOPS = 2 * N * NQ * (D + DV)


def interleave(copy, dst, src):
    copy(dst.rearrange("p (c i) t -> p c t i", i=4), src.rearrange("p t (c i) -> p c t i", i=4))


def quantize(nc, codes, scales, grouped):
    nc.vector.quantize_mx(out=codes.bitcast(FP8X4), scales=scales, in_=grouped.rearrange("p c t -> p (c t)"))


def tile_attend_plo_siggate_topk_kernel(tc, qT, k_words, k_scales, vT, th, og, us, offs, out_0, out_1, out_2):
    nc = tc.nc
    with ExitStack() as ctx:
        sb = ctx.enter_context(tc.tile_pool(name="sb", bufs=1))
        ps = ctx.enter_context(tc.psum_pool(name="ps", bufs=1))
        shared = ctx.enter_context(tc.tile_pool(name="shared", bufs=1))

        def tile(name, shape, dtype):
            return sb.tile(shape, dtype, name=name, tag=name, align_bytes=64)

        def placed(name, shape, dtype, offset):
            return shared.tile(shape, dtype, name=name, tag=name, align_bytes=64, offset=offset)

        def turn_bank(name, shape):
            return ps.tile(shape, F32, name=name, tag="turn", bufs=3)

        halves = [slice(h * HALF, (h + 1) * HALF) for h in range(2)]
        whole = slice(0, NQ)

        offsets = tile("offsets", [P, N // 16], U16)
        ks_pool = tile("ks_pool", [P, T], U8)
        ks = [tile("ks%d" % g, [P, N], U8) for g in range(PASSES)]
        th_rows = tile("th_rows", [P, P], F32)
        ident = tile("ident", [P, P], F32)
        warm_in = tile("warm_in", [P, 1], F32)
        nc.vector.memset(ks_pool[32:64, :].bitcast(I32), 0)
        nc.vector.memset(ks_pool[64:128, :].bitcast(I32), 0)
        nc.vector.memset(ks[0][32:64, :].bitcast(I32), 0)
        nc.vector.memset(ks[0][64:128, :].bitcast(I32), 0)
        nc.vector.memset(ks[1][:].bitcast(I32), 0)
        nc.gpsimd.memset(th_rows[:], 0.0)
        nc.gpsimd.memset(warm_in[:], 0.0)
        make_identity(nc, ident[:])

        q_raw = [tile("q_raw%d" % g, [P, PACK, NQ], F32) for g in range(PASSES)]
        kw_pool = tile("kw_pool", [P, T], I32)
        us_sb = tile("us_sb", [P, PACK], F32)
        v_pool = [placed("v_pool%d" % t, [P, T], F32, POOL_BYTES * t) for t in range(PACK)]
        res = tile("res", [P, PACK, NQ], F32)
        og_sb = [
            placed("og0", [P, 1, NQ], F32, ON_GATE0),
            placed("og1", [P, 1, NQ], F32, ON_GATE1),
            tile("og2", [P, 1, NQ], F32),
            tile("og3", [P, 1, NQ], F32),
        ]
        gates = [tile("gate%d" % t, [P, NQ], F32) for t in range(PACK)]

        nc.sync.dma_start(offsets[:], offs)
        nc.sync.dma_start(ks_pool[0:32, :].bitcast(I32), k_scales.rearrange("o f t -> (o f) t").bitcast(I32))
        nc.sync.dma_start(kw_pool[:], k_words[0].rearrange("p t b -> p (t b)").bitcast(I32))
        nc.scalar.dma_start(th_rows[0:BANDS, :], th[0, 0].rearrange("(j p) -> j p", p=P))

        warm_out = tile("warm_out", [P, 1], F32)
        nc.scalar.activation(warm_out[:], warm_in[:], SIGMOID)

        th_ps = turn_bank("th_ps", [P, P])
        nc.tensor.transpose(th_ps[:], th_rows[:], ident[:])
        neg_th = tile("neg_th", [P, BANDS], F32)
        nc.scalar.activation(neg_th[:], th_ps[:, 0:BANDS], COPY, scale=-1.0)

        ks_picked = tile("ks_picked", [P, N], U8)
        nc.vector.tensor_copy(ks_picked[:], ks_pool[:].indirect(offsets[:]))
        nc.vector.tensor_copy(ks[0][0:32, :].bitcast(I32), ks_picked[0:32, :].bitcast(I32))
        q_rows = qT[0].rearrange("(g p t) q -> g p t q", p=P, t=PACK)
        for g in range(PASSES):
            nc.sync.dma_start(q_raw[g][:], q_rows[g])
            for quad in range(1 - g, QUADS):
                row = 16 * g + 4 * quad
                nc.sync.dma_start(
                    ks[g][32 * quad : 32 * quad + 4, :].bitcast(I32), ks_picked[row : row + 4, :].bitcast(I32)
                )

        v_rows = vT.rearrange("(p t) n -> t p n", t=PACK)
        og_rows = og[0].rearrange("(p t) q -> p t q", t=PACK)
        nc.sync.dma_start(v_pool[0][:], v_rows[0])
        nc.sync.dma_start(us_sb[:], us[0].rearrange("(p r) one -> p (r one)", r=PACK))
        for t in range(1, PACK):
            nc.sync.dma_start(v_pool[t][:], v_rows[t])
        for t in range(PACK):
            nc.sync.dma_start(og_sb[t][:], og_rows[:, t : t + 1, :])

        kw = tile("kw", [P, N], U32)
        nc.vector.tensor_copy(kw[:], kw_pool[:].bitcast(U32).indirect(offsets[:]))
        k_codes = [tile("k_codes%d" % g, [P, 2 * N], U8) for g in range(PASSES)]
        for g in range(PASSES):
            nc.vector.tensor_copy(k_codes[g][:].bitcast(U16), kw[:].bitcast(U16)[:, g : 2 * N : 2])

        q_codes = [[tile("q_codes%d%d" % (g, j), [P, P], U32) for j in range(BANDS)] for g in range(PASSES)]
        q_scales = [[tile("q_scales%d%d" % (g, j), [P, P], U8) for j in range(BANDS)] for g in range(PASSES)]
        for g in range(PASSES):
            q_grp = [tile("q_grp%d%d" % (g, j), [P, P, PACK], BF16) for j in range(BANDS)]
            for j in range(BANDS):
                copy = nc.vector.tensor_copy if j < BANDS // 2 else nc.scalar.copy
                interleave(copy, q_grp[j][:], q_raw[g][:, :, j * P : (j + 1) * P])
            for j in range(BANDS):
                quantize(nc, q_codes[g][j][:], q_scales[g][j][:], q_grp[j][:])

        score = [ps.tile([P, N], F32, name="score%d" % j, tag="acc%d" % j) for j in range(BANDS)]
        for g in range(PASSES):
            for j in range(BANDS):
                nc.tensor.matmul_mx(
                    score[j][:],
                    lhsT=q_codes[g][j][:].bitcast(FP8X4),
                    lhsT_scale=q_scales[g][j][:],
                    rhs=k_codes[g][:].bitcast(FP4X4),
                    rhs_scale=ks[g][:],
                    start=(g == 0),
                    stop=(g == PASSES - 1),
                )

        v_turned = {}
        v_codes = {}
        v_scales = {}

        def v_pick(t):
            picked = tile("v_picked%d" % t, [P, N], BF16)
            nc.vector.tensor_copy(
                picked[:].rearrange("p (u s e) -> p s u e", u=2, e=2), v_pool[t][:].indirect(offsets[:])
            )
            words = picked[:].bitcast(F32)
            v_turned[t] = turn_bank("v_turned%d" % t, [P, 2, P])
            for u in range(2):
                nc.tensor.transpose(v_turned[t][:, u, :], words[:, u * P : (u + 1) * P], ident[:])

        def v_copy(t, grouped):
            nc.scalar.copy(
                grouped.rearrange("p c t -> p (c t)").bitcast(F32).rearrange("p (c u) -> p c u", u=2),
                v_turned[t][:].rearrange("p u c -> p c u"),
            )

        def v_quant(first, count, grouped, codes):
            scales = tile("v_scales%d" % first, [P, count * P], U8)
            quantize(nc, codes[:], scales[:], grouped[:])
            for i in range(count):
                v_codes[first + i] = codes[:, i * P : (i + 1) * P]
                v_scales[first + i] = scales[:, i * P : (i + 1) * P]

        y_grp = tile("y_grp", [P, NQ, PACK], BF16)
        y_turned = {}
        y_codes = {}
        y_scales = {}

        def y_turn(j):
            sig = tile("sig%d" % j, [P, PACK, P], F32)
            nc.scalar.activation(
                sig[:], score[j][:].rearrange("p (s r) -> p r s", r=PACK), SIGMOID, bias=neg_th[:, j : j + 1]
            )
            y_turned[j] = ps.tile([P, PACK, P], F32, name="y_turned%d" % j, tag="acc%d" % j)
            for r in range(PACK):
                nc.tensor.transpose(y_turned[j][:, r, :], sig[:, r, :], ident[:])

        def y_scale_on_vector(j, last):
            nc.vector.tensor_tensor(
                y_grp[:, j * P : j * P + last, :],
                y_turned[j][:, :, 0:last].rearrange("p r q -> p q r"),
                us_sb[:].unsqueeze(1).broadcast_to([P, last, PACK]),
                MULT,
            )

        def y_scale_on_scalar(j, first):
            staged = tile("y_staged%d" % j, [P, PACK, P - first], BF16)
            for r in range(PACK):
                nc.scalar.activation(staged[:, r, :], y_turned[j][:, r, first:P], COPY, scale=us_sb[:, r : r + 1])
            interleave(nc.scalar.copy, y_grp[:, j * P + first : (j + 1) * P, :], staged[:])

        def y_quant(h, codes):
            y_codes[h] = codes
            y_scales[h] = tile("y_scales%d" % h, [P, HALF], U8)
            quantize(nc, codes[:], y_scales[h][:], y_grp[:, halves[h], :])

        def gate_sigmoid(t, cols):
            nc.scalar.activation(gates[t][:, cols], og_sb[t][:, 0, cols], SIGMOID)

        def product(acc, t, h, cols):
            nc.tensor.matmul_mx(
                acc,
                lhsT=v_codes[t].bitcast(FP8X4),
                lhsT_scale=v_scales[t],
                rhs=y_codes[h][:, cols].bitcast(FP8X4),
                rhs_scale=y_scales[h][:, cols],
                start=True,
                stop=True,
            )

        def products(t):
            for h in range(2):
                product(accs[t][:, halves[h]], t, h, slice(0, HALF))

        def gated(t, acc, cols):
            nc.vector.tensor_tensor(res[:, t, cols], acc, gates[t][:, cols], MULT)

        out_rows = out_0.rearrange("(p t) q -> p t q", t=PACK)

        def store(t):
            nc.sync.dma_start(out_rows[:, t, :], res[:, t, :])

        v_pick(0)
        for j in range(2):
            y_turn(j)
            y_scale_on_vector(j, P)
        y_turn(2)
        y_scale_on_vector(2, BAND2_ON_VECTOR)
        y_quant(0, tile("y_codes0", [P, HALF], U32))
        y_turn(3)
        y_scale_on_scalar(2, BAND2_ON_VECTOR)
        y_scale_on_scalar(3, 0)
        v_pick(1)
        accs = [ps.tile([P, NQ], F32, name="o%d" % t, tag="acc%d" % t) for t in range(PACK - 1)]
        v_grp01 = tile("v_grp01", [P, 2 * P, PACK], BF16)
        v_copy(0, v_grp01[:, 0:P, :])
        v_copy(1, v_grp01[:, P : 2 * P, :])

        v_pick(2)
        y_quant(1, placed("y_codes1", [P, HALF], U32, ON_POOL2))
        v_quant(0, 2, v_grp01, placed("v_codes01", [P, 2 * P], U32, ON_POOL2 + HALF * 4))
        products(0)
        products(1)
        v_grp2 = tile("v_grp2", [P, P, PACK], BF16)
        v_copy(2, v_grp2[:])

        v_pick(3)
        gate_sigmoid(0, whole)
        gate_sigmoid(1, whole)
        v_quant(2, 1, v_grp2, placed("v_codes2", [P, P], U32, ON_GATE0))
        products(2)
        for t in range(2):
            gated(t, accs[t][:], whole)
            store(t)

        gate_sigmoid(2, slice(0, GATE2_AHEAD))
        v_grp3 = placed("v_grp3", [P, P, PACK], BF16, ON_GATE1)
        v_copy(3, v_grp3[:])
        gate_sigmoid(2, slice(GATE2_AHEAD, NQ))
        v_quant(3, 1, v_grp3, tile("v_codes3", [P, P], U32))
        for cols in halves:
            gate_sigmoid(3, cols)
        gated(2, accs[2][:], whole)
        store(2)

        pieces = [(0, slice(0, P)), (0, slice(P, HALF)), (1, slice(0, HALF))]
        sums = []
        sums.append(ps.tile([P, P], F32, name="o3_0", tag="acc3"))
        product(sums[0][:], 3, *pieces[0])
        sums.append(turn_bank("o3_1", [P, P]))
        product(sums[1][:], 3, *pieces[1])
        sums.append(ps.tile([P, HALF], F32, name="o3_2", tag="spare"))
        product(sums[2][:], 3, *pieces[2])
        for acc, (h, cols) in zip(sums, pieces):
            gated(3, acc[:], slice(h * HALF + cols.start, h * HALF + cols.stop))
        store(3)

        o_scales = tile("o_scales", [P, NQ], U8)
        words_out = out_1[0].rearrange("p q b -> p (q b)").bitcast(I32)
        o_grp = [tile("o_grp%d" % h, [P, HALF, PACK], BF16) for h in range(2)]
        for pair in (slice(0, 2), slice(2, 4)):
            interleave(nc.scalar.copy, o_grp[0][:, 0:P, pair], res[:, pair, 0:P])
        split = HALF + GROUP_ON_SCALAR
        interleave(nc.scalar.copy, o_grp[1][:, 0:GROUP_ON_SCALAR, :], res[:, :, HALF:split])
        interleave(nc.vector.tensor_copy, o_grp[0][:, P:HALF, :], res[:, :, P:HALF])
        interleave(nc.vector.tensor_copy, o_grp[1][:, GROUP_ON_SCALAR:HALF, :], res[:, :, split:NQ])
        for h in range(2):
            o_codes = tile("o_codes%d" % h, [P, HALF], U32)
            quantize(nc, o_codes[:], o_scales[:, halves[h]], o_grp[h][:])
            nc.sync.dma_start(words_out[:, halves[h]], o_codes[:].bitcast(I32))
        for quad in range(QUADS):
            queue = nc.scalar if quad % 2 == 0 else nc.sync
            queue.dma_start(
                out_2[0, 4 * quad : 4 * quad + 4, :].bitcast(I32),
                o_scales[32 * quad : 32 * quad + 4, :].bitcast(I32),
            )
